import numpy as np
import ml_dtypes


def mxq(x, axis, fmt="e4m3"):
    dtype, down = {"e4m3": (ml_dtypes.float8_e4m3fn, 7), "e5m2": (ml_dtypes.float8_e5m2, 14)}[fmt]
    v = np.moveaxis(np.asarray(x, np.float32).astype(ml_dtypes.bfloat16).astype(np.float64), axis, -1)
    blocks = v.reshape(v.shape[:-1] + (-1, 32))
    amax = np.abs(blocks).max(-1, keepdims=True)
    byte = np.maximum(np.where(amax > 0, np.frexp(amax)[1] - 1 + 127, 0) - down, 1)
    scale = np.exp2(byte - 127.0)
    codes = (blocks / scale).astype(np.float32).astype(dtype).astype(np.float64)
    return np.moveaxis((codes * scale).reshape(v.shape), -1, axis)


WIDE = False


def mx_kscale(k):
    if not WIDE:
        return np.ones(k)
    levels = np.array([10, -10, 5, -5, 0])
    if k % 512:
        return np.exp2(np.random.permutation(np.resize(levels, k // 32))).repeat(32)
    a = np.empty((k // 512, 16))
    for p in range(k // 512):
        a[p, :8] = np.random.permutation(np.resize(levels, 8))
        for g in range(8):
            far = levels[np.abs(levels - a[p, g]) >= 10]
            a[p, g + 8] = far[np.random.randint(len(far))]
    return np.exp2(a.ravel()).repeat(32)


def f64(x):
    return np.asarray(x).astype(np.float64)


def striped(idx):
    return np.tile(idx.reshape(-1, 16).T, (8, 1)).astype(np.uint16)


def unstriped(offs):
    return offs[:16].T.reshape(-1).astype(np.int64)


E2M1 = np.array([0.0, 0.5, 1.0, 1.5, 2.0, 3.0, 4.0, 6.0, -0.0, -0.5, -1.0, -1.5, -2.0, -3.0, -4.0, -6.0])


def pack_fp4(w):
    k, n = w.shape
    w = f64(np.asarray(w, np.float32).astype(ml_dtypes.bfloat16)).reshape(k // 32, 32, n)
    amax = np.abs(w).max(1)
    mant, ex = np.frexp(amax / 6.0)
    byte = np.clip(np.where(amax > 0, np.where(mant > 0.5, ex, ex - 1) + 127, 1), 1, 254)
    scaled = (w * np.exp2(127.0 - byte)[:, None, :]).reshape(k, n).astype(np.float32)
    c = np.ascontiguousarray(scaled.reshape(k // 512, 128, 4, n).transpose(0, 1, 3, 2)).astype(ml_dtypes.float4_e2m1fn).view(np.uint8) & 0xF
    words = (c[..., 0::2] | (c[..., 1::2] << 4)).reshape(k // 512, 128, 2 * n)
    return np.ascontiguousarray(words), np.ascontiguousarray(byte.astype(np.uint8).reshape(k // 512, 16, n))


def unpack_fp4(words, scales):
    g, _, n = scales.shape
    words = np.ascontiguousarray(words).reshape(g, 128, n, 2)
    nib = np.empty((g, 128, n, 4), np.uint8)
    nib[..., 0::2] = words & 0xF
    nib[..., 1::2] = words >> 4
    vals = E2M1[nib] * np.repeat(np.exp2(scales.astype(np.float64) - 127.0), 8, axis=1)[..., None]
    return vals.transpose(0, 1, 3, 2).reshape(g * 512, n)


K, T, S, H, N = 1024, 2048, 1024, 512, 128


def setup_inputs():
    n = np.random.standard_normal
    s = mx_kscale(K)[:, None]
    u = mx_kscale(H)
    packed_w2 = pack_fp4(n((H, N)) / np.sqrt(H) / u[:, None])
    return {
        "xT": (n((K, T)) * s).astype(np.float32),
        "w1": (n((K, H)) / np.sqrt(K) / s * u).astype(np.float32),
        "w2_words": packed_w2[0],
        "w2_scales": packed_w2[1],
        "offs": striped(np.random.permutation(T)[:S]),
    }


def reference(xT, w1, w2_words, w2_scales, offs):
    xq = mxq(f64(xT)[:, unstriped(offs)], 0, "e4m3")
    h = mxq(f64(w1), 0, "e4m3").T @ xq
    z = h - h.mean(axis=1, keepdims=True)
    return unpack_fp4(w2_words, w2_scales).T @ mxq(z, 0, "e4m3")

@@ -1,0 +1,225 @@
+from contextlib import ExitStack
+
+import concourse.mybir as mybir
+
+K, T, S, H, N = 1024, 2048, 1024, 512, 128
+FLOPS = 2 * K * H * S + 2 * H * N * S
+
+F32 = mybir.dt.float32
+BF16 = mybir.dt.bfloat16
+U32 = mybir.dt.uint32
+I32 = mybir.dt.int32
+U16 = mybir.dt.uint16
+U8 = mybir.dt.uint8
+FP8X4 = mybir.dt.float8_e4m3fn_x4
+FP4X4 = mybir.dt.float4_e2m1fn_x4
+ACT = mybir.ActivationFunctionType
+ALU = mybir.AluOpType
+
+P = 128
+PACK = 4
+K_PASS = P * PACK
+PASSES = K // K_PASS
+HALF = 512
+RUN = 4
+
+X_CHUNKS = [[(512, 256), (512, 256), (512, 256), (512, 256)], [(512, 448), (512, 384), (512, 256), (256, 128), (256, 96)]]
+W_CHUNKS = [[(256, 256), (256, 256)], [(256, 256), (256, 256)]]
+Z_CHUNKS = [(0, 256, False), (512, 256, True), (256, 128, False), (768, 256, True), (384, 128, True)]
+
+
+def tile_picked_deepset_none_e_kernel(tc, xT, w1, w2_words, w2_scales, offs, out):
+    nc = tc.nc
+    with ExitStack() as ctx:
+        keep = ctx.enter_context(tc.tile_pool(name="keep", bufs=1))
+        psum = ctx.enter_context(tc.psum_pool(name="psum", bufs=1))
+
+        def sb(shape, dtype, name):
+            return keep.tile(shape, dtype, name=name, tag=name, align_bytes=64)
+
+        offsets = keep.tile([P, S // 16], U16, name="offsets")
+        x_words = [sb([P, T], U32, f"x_words{g}") for g in range(PASSES)]
+        x_bytes = sb([P, T], U8, "x_bytes")
+        w2_plane = sb([P, N], U8, "w2_plane")
+        w2_codes = sb([P, 2 * N], U8, "w2_codes")
+        nc.gpsimd.memset(x_bytes[:].bitcast(U32), 0)
+        nc.gpsimd.memset(w2_plane[:].bitcast(U32), 0)
+
+        x_raw = {}
+        for g in range(PASSES):
+            c0 = 0
+            for n, (width, on_scalar) in enumerate(X_CHUNKS[g]):
+                raw = sb([P, PACK, width], F32, f"x_raw{g}_{n}")
+                rows = xT[g * K_PASS : (g + 1) * K_PASS, c0 : c0 + width]
+                nc.sync.dma_start(out=raw[:], in_=rows.rearrange("(p j) w -> p j w", j=PACK))
+                x_raw[g, n] = raw
+                if g == 0 and n == 0:
+                    nc.sync.dma_start(offsets[:], offs)
+                c0 = c0 + width
+        w_raw = {}
+        for g in range(PASSES):
+            c0 = 0
+            for n, (width, on_scalar) in enumerate(W_CHUNKS[g]):
+                raw = sb([P, PACK, width], F32, f"w_raw{g}_{n}")
+                rows = w1[g * K_PASS : (g + 1) * K_PASS, c0 : c0 + width]
+                nc.sync.dma_start(out=raw[:], in_=rows.rearrange("(p j) w -> p j w", j=PACK))
+                w_raw[g, n] = raw
+                c0 = c0 + width
+        nc.sync.dma_start(out=w2_codes[:].bitcast(I32), in_=w2_words[0].bitcast(I32))
+        for q in range(4):
+            nc.sync.dma_start(
+                out=w2_plane[32 * q : 32 * q + 4, :].bitcast(I32),
+                in_=w2_scales[0, 4 * q : 4 * q + 4, :].bitcast(I32),
+            )
+
+        def move(on_scalar, dst, src):
+            if on_scalar:
+                nc.scalar.activation(out=dst, in_=src, func=ACT.Copy)
+            else:
+                nc.vector.tensor_copy(out=dst, in_=src)
+
+        def interleave(on_scalar, grouped, planes, a, b):
+            if a < b:
+                move(
+                    on_scalar,
+                    grouped[:, a:b, :].rearrange("p (c i) j -> p c j i", i=RUN),
+                    planes[:, :, a:b].rearrange("p j (c i) -> p c j i", i=RUN),
+                )
+
+        picked_words = {}
+        late_words = []
+        picked_bytes = {}
+
+        def gather_words(g, h):
+            if g == 0:
+                dst = sb([P, HALF], U32, f"picked_words{g}_{h}")[:]
+            else:
+                dst = late_words[0][:, HALF * h : HALF * (h + 1)]
+            nc.vector.tensor_copy(dst, x_words[g][:].indirect(offsets[:, 32 * h : 32 * h + 32]))
+            picked_words[g, h] = dst
+
+        def gather_bytes(h):
+            dst = sb([P, HALF], U8, f"picked_bytes{h}")
+            nc.vector.tensor_copy(dst[:], x_bytes[:].indirect(offsets[:, 32 * h : 32 * h + 32]))
+            picked_bytes[h] = dst
+
+        for g in range(PASSES):
+            c0 = 0
+            for n, (width, on_scalar) in enumerate(X_CHUNKS[g]):
+                grouped = sb([P, width, PACK], BF16, f"x_grouped{g}_{n}")
+                interleave(True, grouped, x_raw[g, n], 0, on_scalar)
+                interleave(False, grouped, x_raw[g, n], on_scalar, width)
+                nc.vector.quantize_mx(
+                    out=x_words[g][:, c0 : c0 + width].bitcast(FP8X4),
+                    scales=x_bytes[4 * g : P, c0 : c0 + width],
+                    in_=grouped[:].rearrange("p w j -> p (w j)"),
+                )
+                c0 = c0 + width
+                if g == 1 and n < 2:
+                    gather_words(0, n)
+
+        w_grouped = [sb([P, PACK, P, PACK], BF16, f"w_grouped{g}") for g in range(PASSES)]
+        w_words = [sb([P, H], U32, f"w_words{g}") for g in range(PASSES)]
+        w_bytes = [sb([P, H], U8, f"w_bytes{g}") for g in range(PASSES)]
+
+        def cast_w(g):
+            m0 = 0
+            for n, (width, on_scalar) in enumerate(W_CHUNKS[g]):
+                src = w_raw[g, n][:].rearrange("p j (m t) -> p m j t", t=PACK)
+                dst = w_grouped[g][:].rearrange("p t m j -> p m j t")
+                ms, mw = on_scalar // PACK, width // PACK
+                move(True, dst[:, m0 : m0 + ms], src[:, 0:ms])
+                if ms < mw:
+                    move(False, dst[:, m0 + ms : m0 + mw], src[:, ms:mw])
+                m0 = m0 + mw
+
+        def quantize_w(g, t0, t1):
+            nc.vector.quantize_mx(
+                out=w_words[g][:, P * t0 : P * t1].bitcast(FP8X4),
+                scales=w_bytes[g][:, P * t0 : P * t1],
+                in_=w_grouped[g][:, t0:t1].rearrange("p t m j -> p (t m j)"),
+            )
+
+        banks = {}
+
+        def first_product(g, t, h):
+            if g == 0:
+                banks[t, h] = psum.tile([P, HALF], F32, name=f"h{t}_{h}", tag=f"bank{2 * t + h}")
+            nc.tensor.matmul_mx(
+                out=banks[t, h][:],
+                lhsT=w_words[g][:, P * t : P * (t + 1)].bitcast(FP8X4),
+                lhsT_scale=w_bytes[g][:, P * t : P * (t + 1)],
+                rhs=picked_words[g, h].bitcast(FP8X4),
+                rhs_scale=picked_bytes[h][4 * g : P, :],
+                start=(g == 0),
+                stop=(g == PASSES - 1),
+            )
+
+        cast_w(0)
+        cast_w(1)
+        gather_bytes(0)
+        gather_bytes(1)
+        quantize_w(0, 0, PACK)
+        for h in range(2):
+            for t in range(PACK):
+                first_product(0, t, h)
+        late_words.append(keep.tile([P, S], U32, name="late_words", tag="w_grouped0", align_bytes=64))
+        gather_words(1, 0)
+        gather_words(1, 1)
+
+        h_sb = [sb([P, PACK, HALF], F32, f"h_sb{h}") for h in range(2)]
+        sums = [sb([P, PACK], F32, f"sums{h}") for h in range(2)]
+        neg_mean = sb([P, 1, PACK, 1], F32, "neg_mean")
+        for t in range(PACK):
+            quantize_w(1, t, t + 1)
+        for t in range(PACK):
+            first_product(1, t, 0)
+            first_product(1, t, 1)
+        for t in range(PACK):
+            nc.scalar.activation(out=h_sb[0][:, t, :], in_=banks[t, 0][:], func=ACT.Copy, accum_out=sums[0][:, t : t + 1])
+            nc.vector.tensor_scalar(
+                out=h_sb[1][:, t, :], in0=banks[t, 1][:], scalar1=1.0, scalar2=None,
+                op0=ALU.mult, op1=ALU.add, accum_out=sums[1][:, t : t + 1],
+            )
+            nc.vector.tensor_scalar(
+                out=neg_mean[:, 0, t, :], in0=sums[0][:, t : t + 1], scalar1=sums[1][:, t : t + 1],
+                scalar2=-1.0 / S, op0=ALU.add, op1=ALU.mult,
+            )
+
+        z_grouped = {}
+        z_planes = {}
+        for n, (c0, width, on_scalar) in enumerate(Z_CHUNKS):
+            src = h_sb[c0 // HALF][:, :, c0 % HALF : c0 % HALF + width]
+            z_grouped[n] = sb([P, width, PACK], BF16, f"z_grouped{n}")
+            if on_scalar:
+                z_planes[n] = sb([P, PACK, width], BF16, f"z_planes{n}")
+                for t in range(PACK):
+                    nc.scalar.activation(out=z_planes[n][:, t, :], in_=src[:, t, :], func=ACT.Identity, bias=neg_mean[:, 0, t, :])
+            else:
+                nc.vector.tensor_tensor(
+                    out=z_grouped[n][:].rearrange("p (c i) t -> p c t i", i=RUN),
+                    in0=src.rearrange("p t (c i) -> p c t i", i=RUN),
+                    in1=neg_mean[:].to_broadcast([P, width // RUN, PACK, RUN]),
+                    op=ALU.add,
+                )
+        for n, (c0, width, on_scalar) in enumerate(Z_CHUNKS):
+            if on_scalar:
+                interleave(False, z_grouped[n], z_planes[n], 0, width)
+            z_words = sb([P, width], U32, f"z_words{n}")
+            z_bytes = sb([P, width], U8, f"z_bytes{n}")
+            nc.vector.quantize_mx(
+                out=z_words[:].bitcast(FP8X4), scales=z_bytes[:], in_=z_grouped[n][:].rearrange("p w t -> p (w t)")
+            )
+            result = psum.tile([P, HALF], F32, name=f"result{n}", tag=f"bank{n}")
+            nc.tensor.matmul_mx(
+                out=result[:, 0:width],
+                lhsT=w2_codes[:].bitcast(FP4X4),
+                lhsT_scale=w2_plane[:],
+                rhs=z_words[:].bitcast(FP8X4),
+                rhs_scale=z_bytes[:],
+                start=True,
+                stop=True,
+            )
+            staged = sb([P, width], F32, f"staged{n}")
+            move(True, staged[:], result[:, 0:width])
+            nc.sync.dma_start(out=out[:, c0 : c0 + width], in_=staged[:])

@@ -22,9 +22,10 @@ K_PASS = P * PACK
 PASSES = K // K_PASS
 HALF = 512
 RUN = 4
+WARM = 2
 
-X_CHUNKS = [[(512, 256), (512, 256), (512, 256), (512, 256)], [(512, 448), (512, 384), (512, 256), (256, 128), (256, 96)]]
-W_CHUNKS = [[(256, 256), (256, 256)], [(256, 256), (256, 256)]]
+X_CHUNKS = [[(1024, 0), (1024, 384)], [(1024, 1024), (1024, 384)], [(1024, 1024), (1024, 512)], [(1024, 1024), (512, 0), (512, 192)]]
+W_CHUNKS = [[(256, 256), (256, 256)], [(512, 384)]]
 Z_CHUNKS = [(0, 256, False), (512, 256, True), (256, 128, False), (768, 256, True), (384, 128, True)]
 
 
@@ -38,24 +39,22 @@ def tile_picked_deepset_none_e_kernel(tc, xT, w1, w2_words, w2_scales, offs, out
             return keep.tile(shape, dtype, name=name, tag=name, align_bytes=64)
 
         offsets = keep.tile([P, S // 16], U16, name="offsets")
-        x_words = [sb([P, T], U32, f"x_words{g}") for g in range(PASSES)]
-        x_bytes = sb([P, T], U8, "x_bytes")
         w2_plane = sb([P, N], U8, "w2_plane")
         w2_codes = sb([P, 2 * N], U8, "w2_codes")
-        nc.gpsimd.memset(x_bytes[:].bitcast(U32), 0)
         nc.gpsimd.memset(w2_plane[:].bitcast(U32), 0)
 
         x_raw = {}
         for g in range(PASSES):
-            c0 = 0
-            for n, (width, on_scalar) in enumerate(X_CHUNKS[g]):
-                raw = sb([P, PACK, width], F32, f"x_raw{g}_{n}")
-                rows = xT[g * K_PASS : (g + 1) * K_PASS, c0 : c0 + width]
-                nc.sync.dma_start(out=raw[:], in_=rows.rearrange("(p j) w -> p j w", j=PACK))
-                x_raw[g, n] = raw
-                if g == 0 and n == 0:
-                    nc.sync.dma_start(offsets[:], offs)
-                c0 = c0 + width
+            rows = xT[g * K_PASS : (g + 1) * K_PASS, :].rearrange("(p j) w -> p j w", j=PACK)
+            for u in range(2):
+                c0 = 0
+                for n, (width, on_scalar) in enumerate(X_CHUNKS[2 * g + u]):
+                    raw = sb([P, 2, width], F32, f"x_raw{g}_{u}_{n}")
+                    nc.sync.dma_start(out=raw[:], in_=rows[:, 2 * u : 2 * u + 2, c0 : c0 + width])
+                    x_raw[g, u, n] = raw
+                    if (g, u, n) == (0, 0, 0):
+                        nc.sync.dma_start(offsets[:], offs)
+                    c0 = c0 + width
         w_raw = {}
         for g in range(PASSES):
             c0 = 0
@@ -86,37 +85,54 @@ def tile_picked_deepset_none_e_kernel(tc, xT, w1, w2_words, w2_scales, offs, out
                     planes[:, :, a:b].rearrange("p j (c i) -> p c j i", i=RUN),
                 )
 
-        picked_words = {}
-        late_words = []
-        picked_bytes = {}
-
-        def gather_words(g, h):
-            if g == 0:
-                dst = sb([P, HALF], U32, f"picked_words{g}_{h}")[:]
-            else:
-                dst = late_words[0][:, HALF * h : HALF * (h + 1)]
-            nc.vector.tensor_copy(dst, x_words[g][:].indirect(offsets[:, 32 * h : 32 * h + 32]))
-            picked_words[g, h] = dst
-
-        def gather_bytes(h):
-            dst = sb([P, HALF], U8, f"picked_bytes{h}")
-            nc.vector.tensor_copy(dst[:], x_bytes[:].indirect(offsets[:, 32 * h : 32 * h + 32]))
-            picked_bytes[h] = dst
-
+        x_pairs = {}
+        picked = sb([P, 2, S], U32, "picked")
+        x_words = {}
+        x_bytes = {}
         for g in range(PASSES):
+            for h in range(2):
+                x_words[g, h] = sb([P, HALF], U32, f"x_words{g}_{h}")
+                x_bytes[g, h] = sb([P, HALF], U8, f"x_bytes{g}_{h}")
+
+        def cast_pair(g, u):
+            pairs = sb([P, T, 2], BF16, f"x_pairs{g}_{u}")
+            x_pairs[g, u] = pairs
             c0 = 0
-            for n, (width, on_scalar) in enumerate(X_CHUNKS[g]):
-                grouped = sb([P, width, PACK], BF16, f"x_grouped{g}_{n}")
-                interleave(True, grouped, x_raw[g, n], 0, on_scalar)
-                interleave(False, grouped, x_raw[g, n], on_scalar, width)
-                nc.vector.quantize_mx(
-                    out=x_words[g][:, c0 : c0 + width].bitcast(FP8X4),
-                    scales=x_bytes[4 * g : P, c0 : c0 + width],
-                    in_=grouped[:].rearrange("p w j -> p (w j)"),
-                )
+            for n, (width, on_scalar) in enumerate(X_CHUNKS[2 * g + u]):
+                src = x_raw[g, u, n][:].rearrange("p e w -> p w e")
+                if on_scalar > 0:
+                    move(True, pairs[:, c0 : c0 + on_scalar, :], src[:, 0:on_scalar, :])
+                if on_scalar < width:
+                    move(False, pairs[:, c0 + on_scalar : c0 + width, :], src[:, on_scalar:width, :])
                 c0 = c0 + width
-                if g == 1 and n < 2:
-                    gather_words(0, n)
+
+        def gather(dst, g, u, a, b):
+            window = x_pairs[g, u][:].rearrange("p w e -> p (w e)").bitcast(U32)
+            nc.vector.tensor_copy(dst, window.indirect(offsets[:, a // 16 : b // 16]))
+
+        def weave(dst, a, b):
+            nc.vector.tensor_copy(
+                out=dst.bitcast(I32).rearrange("p (n u) -> p n u", u=2),
+                in_=picked[:, :, a:b].bitcast(I32).rearrange("p u n -> p n u"),
+            )
+
+        def quantize_x(src, g, a, b):
+            h = a // HALF
+            lo, hi = a - HALF * h, b - HALF * h
+            nc.vector.quantize_mx(out=x_words[g, h][:, lo:hi].bitcast(FP8X4), scales=x_bytes[g, h][:, lo:hi], in_=src)
+
+        direct = [sb([P, HALF * PACK], BF16, f"direct{h}") for h in range(2)]
+        for u in range(2):
+            cast_pair(0, u)
+            for h in range(2):
+                slots = direct[h][:].bitcast(U32).rearrange("p (n u) -> p n u", u=2)
+                gather(slots[:, :, u], 0, u, HALF * h, HALF * (h + 1))
+        for h in range(2):
+            quantize_x(direct[h][:], 0, HALF * h, HALF * (h + 1))
+        cast_pair(1, 0)
+        for h in range(2):
+            gather(picked[:, 0, HALF * h : HALF * (h + 1)], 1, 0, HALF * h, HALF * (h + 1))
+        cast_pair(1, 1)
 
         w_grouped = [sb([P, PACK, P, PACK], BF16, f"w_grouped{g}") for g in range(PASSES)]
         w_words = [sb([P, H], U32, f"w_words{g}") for g in range(PASSES)]
@@ -149,23 +165,43 @@ def tile_picked_deepset_none_e_kernel(tc, xT, w1, w2_words, w2_scales, offs, out
                 out=banks[t, h][:],
                 lhsT=w_words[g][:, P * t : P * (t + 1)].bitcast(FP8X4),
                 lhsT_scale=w_bytes[g][:, P * t : P * (t + 1)],
-                rhs=picked_words[g, h].bitcast(FP8X4),
-                rhs_scale=picked_bytes[h][4 * g : P, :],
+                rhs=x_words[g, h][:].bitcast(FP8X4),
+                rhs_scale=x_bytes[g, h][:],
                 start=(g == 0),
                 stop=(g == PASSES - 1),
             )
 
         cast_w(0)
         cast_w(1)
-        gather_bytes(0)
-        gather_bytes(1)
-        quantize_w(0, 0, PACK)
-        for h in range(2):
-            for t in range(PACK):
-                first_product(0, t, h)
-        late_words.append(keep.tile([P, S], U32, name="late_words", tag="w_grouped0", align_bytes=64))
-        gather_words(1, 0)
-        gather_words(1, 1)
+        Q = 256
+        first = sb([P, Q * PACK], BF16, "woven_first")
+        gather(picked[:, 1, 0:Q], 1, 1, 0, Q)
+        gather(picked[:, 1, Q : 2 * Q], 1, 1, Q, 2 * Q)
+        weave(first[:], 0, Q)
+        gather(picked[:, 1, 2 * Q : 3 * Q], 1, 1, 2 * Q, 3 * Q)
+        quantize_x(first[:], 1, 0, Q)
+        gather(picked[:, 1, 3 * Q : 4 * Q], 1, 1, 3 * Q, 4 * Q)
+        warm = psum.tile([P, HALF], F32, name="warm", tag="bank7")
+        for n in range(WARM):
+            nc.tensor.matmul_mx(
+                out=warm[:],
+                lhsT=x_words[1, 0][:, 0:P].bitcast(FP8X4),
+                lhsT_scale=x_bytes[1, 0][:, 0:P],
+                rhs=x_words[0, 0][:].bitcast(FP8X4),
+                rhs_scale=x_bytes[0, 0][:],
+                start=True,
+                stop=True,
+            )
+        for t in range(PACK):
+            quantize_w(0, t, t + 1)
+        for t in range(PACK):
+            first_product(0, t, 1)
+            first_product(0, t, 0)
+        rest = keep.tile([P, 3 * Q * PACK], BF16, name="woven_rest", tag="w_grouped0", align_bytes=64)
+        weave(rest[:, 0 : Q * PACK], Q, 2 * Q)
+        weave(rest[:, Q * PACK : 3 * Q * PACK], 2 * Q, 4 * Q)
+        quantize_x(rest[:, 0 : Q * PACK], 1, Q, 2 * Q)
+        quantize_x(rest[:, Q * PACK : 3 * Q * PACK], 1, 2 * Q, 4 * Q)
 
         h_sb = [sb([P, PACK, HALF], F32, f"h_sb{h}") for h in range(2)]
         sums = [sb([P, PACK], F32, f"sums{h}") for h in range(2)]
@@ -173,18 +209,23 @@ def tile_picked_deepset_none_e_kernel(tc, xT, w1, w2_words, w2_scales, offs, out
         for t in range(PACK):
             quantize_w(1, t, t + 1)
         for t in range(PACK):
-            first_product(1, t, 0)
             first_product(1, t, 1)
+            first_product(1, t, 0)
         for t in range(PACK):
             nc.scalar.activation(out=h_sb[0][:, t, :], in_=banks[t, 0][:], func=ACT.Copy, accum_out=sums[0][:, t : t + 1])
-            nc.vector.tensor_scalar(
-                out=h_sb[1][:, t, :], in0=banks[t, 1][:], scalar1=1.0, scalar2=None,
-                op0=ALU.mult, op1=ALU.add, accum_out=sums[1][:, t : t + 1],
-            )
-            nc.vector.tensor_scalar(
-                out=neg_mean[:, 0, t, :], in0=sums[0][:, t : t + 1], scalar1=sums[1][:, t : t + 1],
-                scalar2=-1.0 / S, op0=ALU.add, op1=ALU.mult,
-            )
+        for t in range(PACK):
+            if t < 4:
+                nc.vector.tensor_scalar(
+                    out=h_sb[1][:, t, :], in0=banks[t, 1][:], scalar1=-1.0 / S, scalar2=None,
+                    op0=ALU.mult, op1=ALU.add, accum_out=sums[1][:, t : t + 1],
+                )
+            else:
+                nc.scalar.activation(
+                    out=h_sb[1][:, t, :], in_=banks[t, 1][:], func=ACT.Copy, scale=-1.0 / S, accum_out=sums[1][:, t : t + 1]
+                )
+        nc.vector.scalar_tensor_tensor(
+            out=neg_mean[:, 0, :, 0], in0=sums[0][:], scalar=-1.0 / S, in1=sums[1][:], op0=ALU.mult, op1=ALU.add
+        )
 
         z_grouped = {}
         z_planes = {}
@@ -194,7 +235,7 @@ def tile_picked_deepset_none_e_kernel(tc, xT, w1, w2_words, w2_scales, offs, out
             if on_scalar:
                 z_planes[n] = sb([P, PACK, width], BF16, f"z_planes{n}")
                 for t in range(PACK):
-                    nc.scalar.activation(out=z_planes[n][:, t, :], in_=src[:, t, :], func=ACT.Identity, bias=neg_mean[:, 0, t, :])
+                    nc.scalar.activation(out=z_planes[n][:, t, :], in_=src[:, t, :], func=ACT.Identity, bias=neg_mean[:, 0, t, :], scale=(1.0 if c0 < HALF else -float(S)))
             else:
                 nc.vector.tensor_tensor(
                     out=z_grouped[n][:].rearrange("p (c i) t -> p c t i", i=RUN),
@@ -222,4 +263,5 @@ def tile_picked_deepset_none_e_kernel(tc, xT, w1, w2_words, w2_scales, offs, out
             )
             staged = sb([P, width], F32, f"staged{n}")
             move(True, staged[:], result[:, 0:width])
-            nc.sync.dma_start(out=out[:, c0 : c0 + width], in_=staged[:])
+            queue = nc.scalar if n == len(Z_CHUNKS) - 1 else nc.sync
+            queue.dma_start(out=out[:, c0 : c0 + width], in_=staged[:])

@@ -23,25 +23,31 @@ PASSES = K // K_PASS
 HALF = 512
 RUN = 4
 WARM = 2
+Q = HALF // 2
+LATE = 16384
 
-X_CHUNKS = [[(1024, 0), (1024, 384)], [(1024, 1024), (1024, 384)], [(1024, 1024), (1024, 512)], [(1024, 1024), (512, 0), (512, 192)]]
-W_CHUNKS = [[(256, 256), (256, 256)], [(512, 384)]]
-Z_CHUNKS = [(0, 256, False), (512, 256, True), (256, 128, False), (768, 256, True), (384, 128, True)]
+X_CHUNKS = [[(1024, 0), (1024, 352)], [(1024, 1024), (1024, 352)], [(1024, 1024), (1024, 512)], [(1024, 832), (768, 192), (256, 96)]]
+W_CHUNKS = [[(256, 256), (256, 256)], [(256, 256), (256, 128)]]
+Z_CHUNKS = [(0, 256, False), (256, 128, False), (512, 256, True), (768, 256, True), (384, 128, True)]
 
 
 def tile_picked_deepset_none_e_kernel(tc, xT, w1, w2_words, w2_scales, offs, out):
     nc = tc.nc
     with ExitStack() as ctx:
         keep = ctx.enter_context(tc.tile_pool(name="keep", bufs=1))
+        shared = ctx.enter_context(tc.tile_pool(name="shared", bufs=1))
         psum = ctx.enter_context(tc.psum_pool(name="psum", bufs=1))
 
         def sb(shape, dtype, name):
             return keep.tile(shape, dtype, name=name, tag=name, align_bytes=64)
 
+        def at(offset, shape, dtype, name):
+            return shared.tile(shape, dtype, name=name, tag=name, align_bytes=64, offset=offset)
+
         offsets = keep.tile([P, S // 16], U16, name="offsets")
         w2_plane = sb([P, N], U8, "w2_plane")
         w2_codes = sb([P, 2 * N], U8, "w2_codes")
-        nc.gpsimd.memset(w2_plane[:].bitcast(U32), 0)
+        nc.vector.memset(w2_plane[:].bitcast(U32), 0)
 
         x_raw = {}
         for g in range(PASSES):
@@ -49,7 +55,10 @@ def tile_picked_deepset_none_e_kernel(tc, xT, w1, w2_words, w2_scales, offs, out
             for u in range(2):
                 c0 = 0
                 for n, (width, on_scalar) in enumerate(X_CHUNKS[2 * g + u]):
-                    raw = sb([P, 2, width], F32, f"x_raw{g}_{u}_{n}")
+                    if (g, u, n) == (1, 1, len(X_CHUNKS[3]) - 1):
+                        raw = at(LATE, [P, 2, width], F32, "x_raw_last")
+                    else:
+                        raw = sb([P, 2, width], F32, f"x_raw{g}_{u}_{n}")
                     nc.sync.dma_start(out=raw[:], in_=rows[:, 2 * u : 2 * u + 2, c0 : c0 + width])
                     x_raw[g, u, n] = raw
                     if (g, u, n) == (0, 0, 0):
@@ -59,7 +68,7 @@ def tile_picked_deepset_none_e_kernel(tc, xT, w1, w2_words, w2_scales, offs, out
         for g in range(PASSES):
             c0 = 0
             for n, (width, on_scalar) in enumerate(W_CHUNKS[g]):
-                raw = sb([P, PACK, width], F32, f"w_raw{g}_{n}")
+                raw = at(20480 + 4096 * (2 * g + n), [P, PACK, width], F32, f"w_raw{g}_{n}")
                 rows = w1[g * K_PASS : (g + 1) * K_PASS, c0 : c0 + width]
                 nc.sync.dma_start(out=raw[:], in_=rows.rearrange("(p j) w -> p j w", j=PACK))
                 w_raw[g, n] = raw
@@ -91,7 +100,8 @@ def tile_picked_deepset_none_e_kernel(tc, xT, w1, w2_words, w2_scales, offs, out
         x_bytes = {}
         for g in range(PASSES):
             for h in range(2):
-                x_words[g, h] = sb([P, HALF], U32, f"x_words{g}_{h}")
+                if g == 0:
+                    x_words[g, h] = sb([P, HALF], U32, f"x_words{g}_{h}")
                 x_bytes[g, h] = sb([P, HALF], U8, f"x_bytes{g}_{h}")
 
         def cast_pair(g, u):
@@ -110,11 +120,17 @@ def tile_picked_deepset_none_e_kernel(tc, xT, w1, w2_words, w2_scales, offs, out
             window = x_pairs[g, u][:].rearrange("p w e -> p (w e)").bitcast(U32)
             nc.vector.tensor_copy(dst, window.indirect(offsets[:, a // 16 : b // 16]))
 
-        def weave(dst, a, b):
-            nc.vector.tensor_copy(
-                out=dst.bitcast(I32).rearrange("p (n u) -> p n u", u=2),
-                in_=picked[:, :, a:b].bitcast(I32).rearrange("p u n -> p n u"),
-            )
+        def weave(on_scalar, dst, a, b):
+            if on_scalar:
+                nc.scalar.copy(
+                    out=dst.bitcast(U32).rearrange("p (n u) -> p n u", u=2),
+                    in_=picked[:, :, a:b].rearrange("p u n -> p n u"),
+                )
+            else:
+                nc.vector.tensor_copy(
+                    out=dst.bitcast(I32).rearrange("p (n u) -> p n u", u=2),
+                    in_=picked[:, :, a:b].bitcast(I32).rearrange("p u n -> p n u"),
+                )
 
         def quantize_x(src, g, a, b):
             h = a // HALF
@@ -127,14 +143,14 @@ def tile_picked_deepset_none_e_kernel(tc, xT, w1, w2_words, w2_scales, offs, out
             for h in range(2):
                 slots = direct[h][:].bitcast(U32).rearrange("p (n u) -> p n u", u=2)
                 gather(slots[:, :, u], 0, u, HALF * h, HALF * (h + 1))
-        for h in range(2):
-            quantize_x(direct[h][:], 0, HALF * h, HALF * (h + 1))
+        quantize_x(direct[0][:], 0, 0, HALF)
+        quantize_x(direct[1][:, 0 : Q * PACK], 0, HALF, HALF + Q)
         cast_pair(1, 0)
         for h in range(2):
             gather(picked[:, 0, HALF * h : HALF * (h + 1)], 1, 0, HALF * h, HALF * (h + 1))
         cast_pair(1, 1)
 
-        w_grouped = [sb([P, PACK, P, PACK], BF16, f"w_grouped{g}") for g in range(PASSES)]
+        w_grouped = [at(6144 * g, [P, PACK, P, PACK], BF16, f"w_grouped{g}") for g in range(PASSES)]
         w_words = [sb([P, H], U32, f"w_words{g}") for g in range(PASSES)]
         w_bytes = [sb([P, H], U8, f"w_bytes{g}") for g in range(PASSES)]
 
@@ -161,60 +177,65 @@ def tile_picked_deepset_none_e_kernel(tc, xT, w1, w2_words, w2_scales, offs, out
         def first_product(g, t, h):
             if g == 0:
                 banks[t, h] = psum.tile([P, HALF], F32, name=f"h{t}_{h}", tag=f"bank{2 * t + h}")
-            nc.tensor.matmul_mx(
-                out=banks[t, h][:],
-                lhsT=w_words[g][:, P * t : P * (t + 1)].bitcast(FP8X4),
-                lhsT_scale=w_bytes[g][:, P * t : P * (t + 1)],
-                rhs=x_words[g, h][:].bitcast(FP8X4),
-                rhs_scale=x_bytes[g, h][:],
-                start=(g == 0),
-                stop=(g == PASSES - 1),
-            )
+            if (g, h) == (0, 1):
+                parts = [(0, Q, x_words[0, 1][:, 0:Q], x_bytes[0, 1][:, 0:Q]), (Q, HALF, late_words[:], late_bytes[:])]
+            else:
+                parts = [(0, HALF, x_words[g, h][:], x_bytes[g, h][:])]
+            for a, b, words, plane in parts:
+                nc.tensor.matmul_mx(
+                    out=banks[t, h][:, a:b],
+                    lhsT=w_words[g][:, P * t : P * (t + 1)].bitcast(FP8X4),
+                    lhsT_scale=w_bytes[g][:, P * t : P * (t + 1)],
+                    rhs=words.bitcast(FP8X4),
+                    rhs_scale=plane,
+                    start=(g == 0 and a == 0),
+                    stop=(g == PASSES - 1),
+                )
 
-        cast_w(0)
-        cast_w(1)
-        Q = 256
-        first = sb([P, Q * PACK], BF16, "woven_first")
-        gather(picked[:, 1, 0:Q], 1, 1, 0, Q)
-        gather(picked[:, 1, Q : 2 * Q], 1, 1, Q, 2 * Q)
-        weave(first[:], 0, Q)
-        gather(picked[:, 1, 2 * Q : 3 * Q], 1, 1, 2 * Q, 3 * Q)
-        quantize_x(first[:], 1, 0, Q)
-        gather(picked[:, 1, 3 * Q : 4 * Q], 1, 1, 3 * Q, 4 * Q)
+        gather(picked[:, 1, 0:HALF], 1, 1, 0, HALF)
+        late_words = at(LATE, [P, Q], U32, "late_words")
+        late_bytes = sb([P, Q], U8, "late_bytes")
+        nc.vector.quantize_mx(out=late_words[:].bitcast(FP8X4), scales=late_bytes[:], in_=direct[1][:, Q * PACK : HALF * PACK])
+        gather(picked[:, 1, HALF:S], 1, 1, HALF, S)
         warm = psum.tile([P, HALF], F32, name="warm", tag="bank7")
         for n in range(WARM):
             nc.tensor.matmul_mx(
                 out=warm[:],
-                lhsT=x_words[1, 0][:, 0:P].bitcast(FP8X4),
-                lhsT_scale=x_bytes[1, 0][:, 0:P],
+                lhsT=late_words[:, 0:P].bitcast(FP8X4),
+                lhsT_scale=late_bytes[:, 0:P],
                 rhs=x_words[0, 0][:].bitcast(FP8X4),
                 rhs_scale=x_bytes[0, 0][:],
                 start=True,
                 stop=True,
             )
+        cast_w(0)
         for t in range(PACK):
             quantize_w(0, t, t + 1)
+        for h in range(2):
+            for t in range(PACK):
+                first_product(0, t, h)
+        woven0 = at(20480 + 4096, [P, HALF * PACK], BF16, "woven0")
+        weave(False, woven0[:], 0, HALF)
+        cast_w(1)
+        woven1 = at(20480 + 3 * 4096, [P, HALF * PACK], BF16, "woven1")
+        weave(True, woven1[:], HALF, S)
+        x_words[1, 0] = sb([P, HALF], U32, "x_words1_0")
+        quantize_x(woven0[:], 1, 0, HALF)
         for t in range(PACK):
-            first_product(0, t, 1)
-            first_product(0, t, 0)
-        rest = keep.tile([P, 3 * Q * PACK], BF16, name="woven_rest", tag="w_grouped0", align_bytes=64)
-        weave(rest[:, 0 : Q * PACK], Q, 2 * Q)
-        weave(rest[:, Q * PACK : 3 * Q * PACK], 2 * Q, 4 * Q)
-        quantize_x(rest[:, 0 : Q * PACK], 1, Q, 2 * Q)
-        quantize_x(rest[:, Q * PACK : 3 * Q * PACK], 1, 2 * Q, 4 * Q)
+            quantize_w(1, t, t + 1)
+        x_words[1, 1] = at(6144, [P, HALF], U32, "x_words1_1")
+        quantize_x(woven1[:], 1, HALF, S)
+        for h in range(2):
+            for t in range(PACK):
+                first_product(1, t, h)
 
         h_sb = [sb([P, PACK, HALF], F32, f"h_sb{h}") for h in range(2)]
         sums = [sb([P, PACK], F32, f"sums{h}") for h in range(2)]
         neg_mean = sb([P, 1, PACK, 1], F32, "neg_mean")
         for t in range(PACK):
-            quantize_w(1, t, t + 1)
-        for t in range(PACK):
-            first_product(1, t, 1)
-            first_product(1, t, 0)
-        for t in range(PACK):
             nc.scalar.activation(out=h_sb[0][:, t, :], in_=banks[t, 0][:], func=ACT.Copy, accum_out=sums[0][:, t : t + 1])
         for t in range(PACK):
-            if t < 4:
+            if t < PACK - 1:
                 nc.vector.tensor_scalar(
                     out=h_sb[1][:, t, :], in0=banks[t, 1][:], scalar1=-1.0 / S, scalar2=None,
                     op0=ALU.mult, op1=ALU.add, accum_out=sums[1][:, t : t + 1],
@@ -223,14 +244,23 @@ def tile_picked_deepset_none_e_kernel(tc, xT, w1, w2_words, w2_scales, offs, out
                 nc.scalar.activation(
                     out=h_sb[1][:, t, :], in_=banks[t, 1][:], func=ACT.Copy, scale=-1.0 / S, accum_out=sums[1][:, t : t + 1]
                 )
-        nc.vector.scalar_tensor_tensor(
-            out=neg_mean[:, 0, :, 0], in0=sums[0][:], scalar=-1.0 / S, in1=sums[1][:], op0=ALU.mult, op1=ALU.add
-        )
+            if t >= PACK - 2:
+                t0 = 0 if t == PACK - 2 else t
+                nc.vector.scalar_tensor_tensor(
+                    out=neg_mean[:, 0, t0 : t + 1, 0], in0=sums[0][:, t0 : t + 1], scalar=-1.0 / S, in1=sums[1][:, t0 : t + 1],
+                    op0=ALU.mult, op1=ALU.add,
+                )
 
         z_grouped = {}
         z_planes = {}
-        for n, (c0, width, on_scalar) in enumerate(Z_CHUNKS):
-            src = h_sb[c0 // HALF][:, :, c0 % HALF : c0 % HALF + width]
+
+        def source(n):
+            c0, width, on_scalar = Z_CHUNKS[n]
+            return h_sb[c0 // HALF][:, :, c0 % HALF : c0 % HALF + width]
+
+        def subtract(n):
+            c0, width, on_scalar = Z_CHUNKS[n]
+            src = source(n)
             z_grouped[n] = sb([P, width, PACK], BF16, f"z_grouped{n}")
             if on_scalar:
                 z_planes[n] = sb([P, PACK, width], BF16, f"z_planes{n}")
@@ -243,9 +273,12 @@ def tile_picked_deepset_none_e_kernel(tc, xT, w1, w2_words, w2_scales, offs, out
                     in1=neg_mean[:].to_broadcast([P, width // RUN, PACK, RUN]),
                     op=ALU.add,
                 )
-        for n, (c0, width, on_scalar) in enumerate(Z_CHUNKS):
-            if on_scalar:
-                interleave(False, z_grouped[n], z_planes[n], 0, width)
+
+        def lay(n):
+            interleave(False, z_grouped[n], z_planes[n], 0, Z_CHUNKS[n][1])
+
+        def second_product(n):
+            c0, width, on_scalar = Z_CHUNKS[n]
             z_words = sb([P, width], U32, f"z_words{n}")
             z_bytes = sb([P, width], U8, f"z_bytes{n}")
             nc.vector.quantize_mx(
@@ -265,3 +298,14 @@ def tile_picked_deepset_none_e_kernel(tc, xT, w1, w2_words, w2_scales, offs, out
             move(True, staged[:], result[:, 0:width])
             queue = nc.scalar if n == len(Z_CHUNKS) - 1 else nc.sync
             queue.dma_start(out=out[:, c0 : c0 + width], in_=staged[:])
+
+        for n in range(len(Z_CHUNKS)):
+            subtract(n)
+        second_product(0)
+        lay(2)
+        lay(3)
+        second_product(2)
+        second_product(3)
+        lay(4)
+        second_product(1)
+        second_product(4)

@@ -27,7 +27,7 @@ Q = HALF // 2
 LATE = 16384
 
 X_CHUNKS = [[(1024, 0), (1024, 352)], [(1024, 1024), (1024, 352)], [(1024, 1024), (1024, 512)], [(1024, 832), (768, 192), (256, 96)]]
-W_CHUNKS = [[(256, 256), (256, 256)], [(256, 256), (256, 128)]]
+W_CHUNKS = [[(256, (True, True)), (256, (True, True))], [(256, (True, True)), (256, (True, False))]]
 Z_CHUNKS = [(0, 256, False), (256, 128, False), (512, 256, True), (768, 256, True), (384, 128, True)]
 
 
@@ -95,7 +95,8 @@ def tile_picked_deepset_none_e_kernel(tc, xT, w1, w2_words, w2_scales, offs, out
                 )
 
         x_pairs = {}
-        picked = sb([P, 2, S], U32, "picked")
+        picked_row = sb([P, 2 * S + Q], U32, "picked_row")
+        picked = picked_row[:, 0 : 2 * S].rearrange("p (u n) -> p u n", u=2)
         x_words = {}
         x_bytes = {}
         for g in range(PASSES):
@@ -150,7 +151,9 @@ def tile_picked_deepset_none_e_kernel(tc, xT, w1, w2_words, w2_scales, offs, out
             gather(picked[:, 0, HALF * h : HALF * (h + 1)], 1, 0, HALF * h, HALF * (h + 1))
         cast_pair(1, 1)
 
-        w_grouped = [at(6144 * g, [P, PACK, P, PACK], BF16, f"w_grouped{g}") for g in range(PASSES)]
+        w_grouped = {(g, q): at(6144 * g + 2048 * q, [P, 2, P, PACK], BF16, f"w_grouped{g}_{q}") for g in range(PASSES) for q in range(2) if (g, q) != (0, 0)}
+        w_grouped = {key: tile[:] for key, tile in w_grouped.items()}
+        w_grouped[0, 0] = picked_row[:, 2 * S - Q : 2 * S + Q].bitcast(BF16).rearrange("p (t m j) -> p t m j", t=2, j=PACK)
         w_words = [sb([P, H], U32, f"w_words{g}") for g in range(PASSES)]
         w_bytes = [sb([P, H], U8, f"w_bytes{g}") for g in range(PASSES)]
 
@@ -158,18 +161,17 @@ def tile_picked_deepset_none_e_kernel(tc, xT, w1, w2_words, w2_scales, offs, out
             m0 = 0
             for n, (width, on_scalar) in enumerate(W_CHUNKS[g]):
                 src = w_raw[g, n][:].rearrange("p j (m t) -> p m j t", t=PACK)
-                dst = w_grouped[g][:].rearrange("p t m j -> p m j t")
-                ms, mw = on_scalar // PACK, width // PACK
-                move(True, dst[:, m0 : m0 + ms], src[:, 0:ms])
-                if ms < mw:
-                    move(False, dst[:, m0 + ms : m0 + mw], src[:, ms:mw])
+                mw = width // PACK
+                for q in range(2):
+                    dst = w_grouped[g, q].rearrange("p t m j -> p m j t")
+                    move(on_scalar[q], dst[:, m0 : m0 + mw], src[:, :, :, 2 * q : 2 * q + 2])
                 m0 = m0 + mw
 
         def quantize_w(g, t0, t1):
             nc.vector.quantize_mx(
                 out=w_words[g][:, P * t0 : P * t1].bitcast(FP8X4),
                 scales=w_bytes[g][:, P * t0 : P * t1],
-                in_=w_grouped[g][:, t0:t1].rearrange("p t m j -> p (t m j)"),
+                in_=w_grouped[g, t0 // 2][:, t0 % 2 : t0 % 2 + t1 - t0].rearrange("p t m j -> p (t m j)"),
             )
 
         banks = {}
@@ -196,7 +198,7 @@ def tile_picked_deepset_none_e_kernel(tc, xT, w1, w2_words, w2_scales, offs, out
         late_words = at(LATE, [P, Q], U32, "late_words")
         late_bytes = sb([P, Q], U8, "late_bytes")
         nc.vector.quantize_mx(out=late_words[:].bitcast(FP8X4), scales=late_bytes[:], in_=direct[1][:, Q * PACK : HALF * PACK])
-        gather(picked[:, 1, HALF:S], 1, 1, HALF, S)
+        gather(picked[:, 1, HALF : HALF + Q], 1, 1, HALF, HALF + Q)
         warm = psum.tile([P, HALF], F32, name="warm", tag="bank7")
         for n in range(WARM):
             nc.tensor.matmul_mx(
@@ -209,7 +211,9 @@ def tile_picked_deepset_none_e_kernel(tc, xT, w1, w2_words, w2_scales, offs, out
                 stop=True,
             )
         cast_w(0)
-        for t in range(PACK):
+        quantize_w(0, 0, 1)
+        gather(picked[:, 1, HALF + Q : S], 1, 1, HALF + Q, S)
+        for t in range(1, PACK):
             quantize_w(0, t, t + 1)
         for h in range(2):
             for t in range(PACK):
@@ -217,13 +221,13 @@ def tile_picked_deepset_none_e_kernel(tc, xT, w1, w2_words, w2_scales, offs, out
         woven0 = at(20480 + 4096, [P, HALF * PACK], BF16, "woven0")
         weave(False, woven0[:], 0, HALF)
         cast_w(1)
-        woven1 = at(20480 + 3 * 4096, [P, HALF * PACK], BF16, "woven1")
+        woven1 = at(20480 + 2 * 4096, [P, HALF * PACK], BF16, "woven1")
         weave(True, woven1[:], HALF, S)
         x_words[1, 0] = sb([P, HALF], U32, "x_words1_0")
         quantize_x(woven0[:], 1, 0, HALF)
         for t in range(PACK):
             quantize_w(1, t, t + 1)
-        x_words[1, 1] = at(6144, [P, HALF], U32, "x_words1_1")
+        x_words[1, 1] = at(6144 + 2048, [P, HALF], U32, "x_words1_1")
         quantize_x(woven1[:], 1, HALF, S)
         for h in range(2):
             for t in range(PACK):

@@ -22,7 +22,6 @@ K_PASS = P * PACK
 PASSES = K // K_PASS
 HALF = 512
 RUN = 4
-WARM = 2
 Q = HALF // 2
 LATE = 16384
 
@@ -199,17 +198,6 @@ def tile_picked_deepset_none_e_kernel(tc, xT, w1, w2_words, w2_scales, offs, out
         late_bytes = sb([P, Q], U8, "late_bytes")
         nc.vector.quantize_mx(out=late_words[:].bitcast(FP8X4), scales=late_bytes[:], in_=direct[1][:, Q * PACK : HALF * PACK])
         gather(picked[:, 1, HALF : HALF + Q], 1, 1, HALF, HALF + Q)
-        warm = psum.tile([P, HALF], F32, name="warm", tag="bank7")
-        for n in range(WARM):
-            nc.tensor.matmul_mx(
-                out=warm[:],
-                lhsT=late_words[:, 0:P].bitcast(FP8X4),
-                lhsT_scale=late_bytes[:, 0:P],
-                rhs=x_words[0, 0][:].bitcast(FP8X4),
-                rhs_scale=x_bytes[0, 0][:],
-                start=True,
-                stop=True,
-            )
         cast_w(0)
         quantize_w(0, 0, 1)
         gather(picked[:, 1, HALF + Q : S], 1, 1, HALF + Q, S)

@@ -22,11 +22,9 @@ K_PASS = P * PACK
 PASSES = K // K_PASS
 HALF = 512
 RUN = 4
-Q = HALF // 2
-LATE = 16384
+W_LOAD = 256
 
-X_CHUNKS = [[(1024, 0), (1024, 352)], [(1024, 1024), (1024, 352)], [(1024, 1024), (1024, 512)], [(1024, 832), (768, 192), (256, 96)]]
-W_CHUNKS = [[(256, (True, True)), (256, (True, True))], [(256, (True, True)), (256, (True, False))]]
+X_CHUNKS = [[(1024, 0), (1024, 320)], [(1024, 1024), (768, 0), (256, 96)], [(512, 512), (512, 512), (512, 512), (512, 512)], [(512, 512), (512, 512), (512, 256), (256, 0), (256, 96)]]
 Z_CHUNKS = [(0, 256, False), (256, 128, False), (512, 256, True), (768, 256, True), (384, 128, True)]
 
 
@@ -54,10 +52,7 @@ def tile_picked_deepset_none_e_kernel(tc, xT, w1, w2_words, w2_scales, offs, out
             for u in range(2):
                 c0 = 0
                 for n, (width, on_scalar) in enumerate(X_CHUNKS[2 * g + u]):
-                    if (g, u, n) == (1, 1, len(X_CHUNKS[3]) - 1):
-                        raw = at(LATE, [P, 2, width], F32, "x_raw_last")
-                    else:
-                        raw = sb([P, 2, width], F32, f"x_raw{g}_{u}_{n}")
+                    raw = sb([P, 2, width], F32, f"x_raw{g}_{u}_{n}")
                     nc.sync.dma_start(out=raw[:], in_=rows[:, 2 * u : 2 * u + 2, c0 : c0 + width])
                     x_raw[g, u, n] = raw
                     if (g, u, n) == (0, 0, 0):
@@ -65,13 +60,11 @@ def tile_picked_deepset_none_e_kernel(tc, xT, w1, w2_words, w2_scales, offs, out
                     c0 = c0 + width
         w_raw = {}
         for g in range(PASSES):
-            c0 = 0
-            for n, (width, on_scalar) in enumerate(W_CHUNKS[g]):
-                raw = at(20480 + 4096 * (2 * g + n), [P, PACK, width], F32, f"w_raw{g}_{n}")
-                rows = w1[g * K_PASS : (g + 1) * K_PASS, c0 : c0 + width]
+            for n in range(H // W_LOAD):
+                raw = sb([P, PACK, W_LOAD], F32, f"w_raw{g}_{n}")
+                rows = w1[g * K_PASS : (g + 1) * K_PASS, n * W_LOAD : (n + 1) * W_LOAD]
                 nc.sync.dma_start(out=raw[:], in_=rows.rearrange("(p j) w -> p j w", j=PACK))
                 w_raw[g, n] = raw
-                c0 = c0 + width
         nc.sync.dma_start(out=w2_codes[:].bitcast(I32), in_=w2_words[0].bitcast(I32))
         for q in range(4):
             nc.sync.dma_start(
@@ -85,24 +78,11 @@ def tile_picked_deepset_none_e_kernel(tc, xT, w1, w2_words, w2_scales, offs, out
             else:
                 nc.vector.tensor_copy(out=dst, in_=src)
 
-        def interleave(on_scalar, grouped, planes, a, b):
-            if a < b:
-                move(
-                    on_scalar,
-                    grouped[:, a:b, :].rearrange("p (c i) j -> p c j i", i=RUN),
-                    planes[:, :, a:b].rearrange("p j (c i) -> p c j i", i=RUN),
-                )
-
         x_pairs = {}
-        picked_row = sb([P, 2 * S + Q], U32, "picked_row")
-        picked = picked_row[:, 0 : 2 * S].rearrange("p (u n) -> p u n", u=2)
+        picked = [sb([P, 2, S], U32, f"picked{g}") for g in range(PASSES)]
+        woven = {}
         x_words = {}
-        x_bytes = {}
-        for g in range(PASSES):
-            for h in range(2):
-                if g == 0:
-                    x_words[g, h] = sb([P, HALF], U32, f"x_words{g}_{h}")
-                x_bytes[g, h] = sb([P, HALF], U8, f"x_bytes{g}_{h}")
+        x_bytes = {(g, h): sb([P, HALF], U8, f"x_bytes{g}_{h}") for g in range(PASSES) for h in range(2)}
 
         def cast_pair(g, u):
             pairs = sb([P, T, 2], BF16, f"x_pairs{g}_{u}")
@@ -116,61 +96,50 @@ def tile_picked_deepset_none_e_kernel(tc, xT, w1, w2_words, w2_scales, offs, out
                     move(False, pairs[:, c0 + on_scalar : c0 + width, :], src[:, on_scalar:width, :])
                 c0 = c0 + width
 
-        def gather(dst, g, u, a, b):
+        def gather(g, u, a, b):
             window = x_pairs[g, u][:].rearrange("p w e -> p (w e)").bitcast(U32)
-            nc.vector.tensor_copy(dst, window.indirect(offsets[:, a // 16 : b // 16]))
+            nc.vector.tensor_copy(picked[g][:, u, a:b], window.indirect(offsets[:, a // 16 : b // 16]))
 
-        def weave(on_scalar, dst, a, b):
-            if on_scalar:
-                nc.scalar.copy(
-                    out=dst.bitcast(U32).rearrange("p (n u) -> p n u", u=2),
-                    in_=picked[:, :, a:b].rearrange("p u n -> p n u"),
-                )
-            else:
-                nc.vector.tensor_copy(
-                    out=dst.bitcast(I32).rearrange("p (n u) -> p n u", u=2),
-                    in_=picked[:, :, a:b].bitcast(I32).rearrange("p u n -> p n u"),
-                )
+        def weave(g, h):
+            nc.vector.tensor_copy(
+                out=woven[g, h][:].bitcast(I32).rearrange("p (n u) -> p n u", u=2),
+                in_=picked[g][:, :, HALF * h : HALF * (h + 1)].bitcast(I32).rearrange("p u n -> p n u"),
+            )
 
-        def quantize_x(src, g, a, b):
-            h = a // HALF
-            lo, hi = a - HALF * h, b - HALF * h
-            nc.vector.quantize_mx(out=x_words[g, h][:, lo:hi].bitcast(FP8X4), scales=x_bytes[g, h][:, lo:hi], in_=src)
+        def quantize_x(g, h):
+            nc.vector.quantize_mx(out=x_words[g, h][:].bitcast(FP8X4), scales=x_bytes[g, h][:], in_=woven[g, h][:])
 
-        direct = [sb([P, HALF * PACK], BF16, f"direct{h}") for h in range(2)]
+        for h in range(2):
+            woven[0, h] = sb([P, HALF * PACK], BF16, f"woven0_{h}")
+            x_words[0, h] = sb([P, HALF], U32, f"x_words0_{h}")
         for u in range(2):
             cast_pair(0, u)
-            for h in range(2):
-                slots = direct[h][:].bitcast(U32).rearrange("p (n u) -> p n u", u=2)
-                gather(slots[:, :, u], 0, u, HALF * h, HALF * (h + 1))
-        quantize_x(direct[0][:], 0, 0, HALF)
-        quantize_x(direct[1][:, 0 : Q * PACK], 0, HALF, HALF + Q)
-        cast_pair(1, 0)
+            gather(0, u, 0, S)
         for h in range(2):
-            gather(picked[:, 0, HALF * h : HALF * (h + 1)], 1, 0, HALF * h, HALF * (h + 1))
+            weave(0, h)
+        for h in range(2):
+            quantize_x(0, h)
+        cast_pair(1, 0)
+        gather(1, 0, 0, S)
         cast_pair(1, 1)
+        for h in range(2):
+            gather(1, 1, HALF * h, HALF * (h + 1))
 
-        w_grouped = {(g, q): at(6144 * g + 2048 * q, [P, 2, P, PACK], BF16, f"w_grouped{g}_{q}") for g in range(PASSES) for q in range(2) if (g, q) != (0, 0)}
-        w_grouped = {key: tile[:] for key, tile in w_grouped.items()}
-        w_grouped[0, 0] = picked_row[:, 2 * S - Q : 2 * S + Q].bitcast(BF16).rearrange("p (t m j) -> p t m j", t=2, j=PACK)
+        w_grouped = {(g, q): at(8192 * g + 4096 * q, [P, 2, P, PACK], BF16, f"w_grouped{g}_{q}") for g in range(PASSES) for q in range(2)}
         w_words = [sb([P, H], U32, f"w_words{g}") for g in range(PASSES)]
         w_bytes = [sb([P, H], U8, f"w_bytes{g}") for g in range(PASSES)]
 
-        def cast_w(g):
-            m0 = 0
-            for n, (width, on_scalar) in enumerate(W_CHUNKS[g]):
-                src = w_raw[g, n][:].rearrange("p j (m t) -> p m j t", t=PACK)
-                mw = width // PACK
-                for q in range(2):
-                    dst = w_grouped[g, q].rearrange("p t m j -> p m j t")
-                    move(on_scalar[q], dst[:, m0 : m0 + mw], src[:, :, :, 2 * q : 2 * q + 2])
-                m0 = m0 + mw
+        def cast_w(g, n, q, on_scalar):
+            src = w_raw[g, n][:].rearrange("p j (m t) -> p m j t", t=PACK)
+            mw = W_LOAD // PACK
+            dst = w_grouped[g, q][:].rearrange("p t m j -> p m j t")
+            move(on_scalar, dst[:, mw * n : mw * (n + 1)], src[:, :, :, 2 * q : 2 * q + 2])
 
-        def quantize_w(g, t0, t1):
+        def quantize_w(g, q):
             nc.vector.quantize_mx(
-                out=w_words[g][:, P * t0 : P * t1].bitcast(FP8X4),
-                scales=w_bytes[g][:, P * t0 : P * t1],
-                in_=w_grouped[g, t0 // 2][:, t0 % 2 : t0 % 2 + t1 - t0].rearrange("p t m j -> p (t m j)"),
+                out=w_words[g][:, 2 * P * q : 2 * P * (q + 1)].bitcast(FP8X4),
+                scales=w_bytes[g][:, 2 * P * q : 2 * P * (q + 1)],
+                in_=w_grouped[g, q][:].rearrange("p t m j -> p (t m j)"),
             )
 
         banks = {}
@@ -178,48 +147,40 @@ def tile_picked_deepset_none_e_kernel(tc, xT, w1, w2_words, w2_scales, offs, out
         def first_product(g, t, h):
             if g == 0:
                 banks[t, h] = psum.tile([P, HALF], F32, name=f"h{t}_{h}", tag=f"bank{2 * t + h}")
-            if (g, h) == (0, 1):
-                parts = [(0, Q, x_words[0, 1][:, 0:Q], x_bytes[0, 1][:, 0:Q]), (Q, HALF, late_words[:], late_bytes[:])]
-            else:
-                parts = [(0, HALF, x_words[g, h][:], x_bytes[g, h][:])]
-            for a, b, words, plane in parts:
-                nc.tensor.matmul_mx(
-                    out=banks[t, h][:, a:b],
-                    lhsT=w_words[g][:, P * t : P * (t + 1)].bitcast(FP8X4),
-                    lhsT_scale=w_bytes[g][:, P * t : P * (t + 1)],
-                    rhs=words.bitcast(FP8X4),
-                    rhs_scale=plane,
-                    start=(g == 0 and a == 0),
-                    stop=(g == PASSES - 1),
-                )
+            nc.tensor.matmul_mx(
+                out=banks[t, h][:],
+                lhsT=w_words[g][:, P * t : P * (t + 1)].bitcast(FP8X4),
+                lhsT_scale=w_bytes[g][:, P * t : P * (t + 1)],
+                rhs=x_words[g, h][:].bitcast(FP8X4),
+                rhs_scale=x_bytes[g, h][:],
+                start=(g == 0),
+                stop=(g == PASSES - 1),
+            )
 
-        gather(picked[:, 1, 0:HALF], 1, 1, 0, HALF)
-        late_words = at(LATE, [P, Q], U32, "late_words")
-        late_bytes = sb([P, Q], U8, "late_bytes")
-        nc.vector.quantize_mx(out=late_words[:].bitcast(FP8X4), scales=late_bytes[:], in_=direct[1][:, Q * PACK : HALF * PACK])
-        gather(picked[:, 1, HALF : HALF + Q], 1, 1, HALF, HALF + Q)
-        cast_w(0)
-        quantize_w(0, 0, 1)
-        gather(picked[:, 1, HALF + Q : S], 1, 1, HALF + Q, S)
-        for t in range(1, PACK):
-            quantize_w(0, t, t + 1)
-        for h in range(2):
-            for t in range(PACK):
-                first_product(0, t, h)
-        woven0 = at(20480 + 4096, [P, HALF * PACK], BF16, "woven0")
-        weave(False, woven0[:], 0, HALF)
-        cast_w(1)
-        woven1 = at(20480 + 2 * 4096, [P, HALF * PACK], BF16, "woven1")
-        weave(True, woven1[:], HALF, S)
-        x_words[1, 0] = sb([P, HALF], U32, "x_words1_0")
-        quantize_x(woven0[:], 1, 0, HALF)
+        cast_w(0, 0, 0, True)
+        cast_w(0, 0, 1, True)
+        cast_w(0, 1, 0, True)
+        cast_w(0, 1, 1, True)
+        for q in range(2):
+            quantize_w(0, q)
+            woven[1, q] = at(4096 * q, [P, HALF * PACK], BF16, f"woven1_{q}")
+            weave(1, q)
         for t in range(PACK):
-            quantize_w(1, t, t + 1)
-        x_words[1, 1] = at(6144 + 2048, [P, HALF], U32, "x_words1_1")
-        quantize_x(woven1[:], 1, HALF, S)
-        for h in range(2):
-            for t in range(PACK):
-                first_product(1, t, h)
+            for h in range(2):
+                first_product(0, t, h)
+        for n in range(2):
+            for q in range(2):
+                cast_w(1, n, q, True)
+        x_words[1, 0] = sb([P, HALF], U32, "x_words1_0")
+        quantize_x(1, 0)
+        quantize_w(1, 0)
+        x_words[1, 1] = at(8192, [P, HALF], U32, "x_words1_1")
+        quantize_x(1, 1)
+        quantize_w(1, 1)
+        for q in range(2):
+            for h in range(2):
+                for t in range(2 * q, 2 * q + 2):
+                    first_product(1, t, h)
 
         h_sb = [sb([P, PACK, HALF], F32, f"h_sb{h}") for h in range(2)]
         sums = [sb([P, PACK], F32, f"sums{h}") for h in range(2)]
@@ -267,7 +228,10 @@ def tile_picked_deepset_none_e_kernel(tc, xT, w1, w2_words, w2_scales, offs, out
                 )
 
         def lay(n):
-            interleave(False, z_grouped[n], z_planes[n], 0, Z_CHUNKS[n][1])
+            nc.vector.tensor_copy(
+                out=z_grouped[n][:].rearrange("p (c i) j -> p c j i", i=RUN),
+                in_=z_planes[n][:].rearrange("p j (c i) -> p c j i", i=RUN),
+            )
 
         def second_product(n):
             c0, width, on_scalar = Z_CHUNKS[n]

@@ -22,9 +22,13 @@ K_PASS = P * PACK
 PASSES = K // K_PASS
 HALF = 512
 RUN = 4
-W_LOAD = 256
+LATE = 128
+Q = 256
+ON_VECTOR = ((3, 0), (0, 1), (2, 1))
+WARM = 2
 
-X_CHUNKS = [[(1024, 0), (1024, 320)], [(1024, 1024), (768, 0), (256, 96)], [(512, 512), (512, 512), (512, 512), (512, 512)], [(512, 512), (512, 512), (512, 256), (256, 0), (256, 96)]]
+X_CHUNKS = [[(1024, 0), (1024, 320)], [(1024, 1024), (1024, 352)], [(1024, 1024), (1024, 704)], [(768, 768), (768, 512), (512, 160)]]
+W_LOADS = [[256, 256], [256, 256]]
 Z_CHUNKS = [(0, 256, False), (256, 128, False), (512, 256, True), (768, 256, True), (384, 128, True)]
 
 
@@ -47,24 +51,40 @@ def tile_picked_deepset_none_e_kernel(tc, xT, w1, w2_words, w2_scales, offs, out
         nc.vector.memset(w2_plane[:].bitcast(U32), 0)
 
         x_raw = {}
-        for g in range(PASSES):
-            rows = xT[g * K_PASS : (g + 1) * K_PASS, :].rearrange("(p j) w -> p j w", j=PACK)
-            for u in range(2):
-                c0 = 0
-                for n, (width, on_scalar) in enumerate(X_CHUNKS[2 * g + u]):
-                    raw = sb([P, 2, width], F32, f"x_raw{g}_{u}_{n}")
-                    nc.sync.dma_start(out=raw[:], in_=rows[:, 2 * u : 2 * u + 2, c0 : c0 + width])
-                    x_raw[g, u, n] = raw
-                    if (g, u, n) == (0, 0, 0):
-                        nc.sync.dma_start(offsets[:], offs)
-                    c0 = c0 + width
         w_raw = {}
-        for g in range(PASSES):
-            for n in range(H // W_LOAD):
-                raw = sb([P, PACK, W_LOAD], F32, f"w_raw{g}_{n}")
-                rows = w1[g * K_PASS : (g + 1) * K_PASS, n * W_LOAD : (n + 1) * W_LOAD]
+
+        def load_pair(g, u):
+            rows = xT[g * K_PASS : (g + 1) * K_PASS, :].rearrange("(p j) w -> p j w", j=PACK)
+            c0 = 0
+            for n, (width, on_scalar) in enumerate(X_CHUNKS[2 * g + u]):
+                if (g, u, n) == (1, 1, len(X_CHUNKS[3]) - 1):
+                    raw = at(0, [P, 2, width], F32, "x_raw_last")
+                else:
+                    raw = sb([P, 2, width], F32, f"x_raw{g}_{u}_{n}")
+                nc.sync.dma_start(out=raw[:], in_=rows[:, 2 * u : 2 * u + 2, c0 : c0 + width])
+                x_raw[g, u, n] = raw
+                if (g, u, n) == (0, 0, 0):
+                    nc.sync.dma_start(offsets[:], offs)
+                c0 = c0 + width
+
+        def load_w(g):
+            c0 = 0
+            for n, width in enumerate(W_LOADS[g]):
+                if n == 1:
+                    raw = at(4096 + 4096 * g, [P, PACK, width], F32, f"w_raw{g}_{n}")
+                else:
+                    raw = sb([P, PACK, width], F32, f"w_raw{g}_{n}")
+                rows = w1[g * K_PASS : (g + 1) * K_PASS, c0 : c0 + width]
                 nc.sync.dma_start(out=raw[:], in_=rows.rearrange("(p j) w -> p j w", j=PACK))
                 w_raw[g, n] = raw
+                c0 = c0 + width
+
+        load_pair(0, 0)
+        load_pair(0, 1)
+        load_pair(1, 0)
+        load_pair(1, 1)
+        load_w(0)
+        load_w(1)
         nc.sync.dma_start(out=w2_codes[:].bitcast(I32), in_=w2_words[0].bitcast(I32))
         for q in range(4):
             nc.sync.dma_start(
@@ -79,10 +99,16 @@ def tile_picked_deepset_none_e_kernel(tc, xT, w1, w2_words, w2_scales, offs, out
                 nc.vector.tensor_copy(out=dst, in_=src)
 
         x_pairs = {}
-        picked = [sb([P, 2, S], U32, f"picked{g}") for g in range(PASSES)]
-        woven = {}
+        direct = sb([P, S * PACK], BF16, "direct")
+        picked = sb([P, 2, S], U32, "picked")
+        woven = {(0, h): direct[:, PACK * HALF * h : PACK * HALF * (h + 1)] for h in range(2)}
         x_words = {}
         x_bytes = {(g, h): sb([P, HALF], U8, f"x_bytes{g}_{h}") for g in range(PASSES) for h in range(2)}
+        area = sb([P, (HALF + P) * PACK], BF16, "area")
+        w_grouped = {(g, q): sb([P, 2, P, PACK], BF16, f"w_grouped{g}_{q}")[:] for g in range(PASSES) for q in range(2) if (g, q) != (0, 0)}
+        w_grouped[0, 0] = area[:, (HALF - P) * PACK :].rearrange("p (t m j) -> p t m j", t=2, j=PACK)
+        w_words = [sb([P, H], U32, f"w_words{g}") for g in range(PASSES)]
+        w_bytes = [sb([P, H], U8, f"w_bytes{g}") for g in range(PASSES)]
 
         def cast_pair(g, u):
             pairs = sb([P, T, 2], BF16, f"x_pairs{g}_{u}")
@@ -98,48 +124,32 @@ def tile_picked_deepset_none_e_kernel(tc, xT, w1, w2_words, w2_scales, offs, out
 
         def gather(g, u, a, b):
             window = x_pairs[g, u][:].rearrange("p w e -> p (w e)").bitcast(U32)
-            nc.vector.tensor_copy(picked[g][:, u, a:b], window.indirect(offsets[:, a // 16 : b // 16]))
+            if g == 0:
+                dst = direct[:].bitcast(U32).rearrange("p (n u) -> p n u", u=2)[:, a:b, u]
+            else:
+                dst = picked[:, u, a:b]
+            nc.vector.tensor_copy(dst, window.indirect(offsets[:, a // 16 : b // 16]))
 
-        def weave(g, h):
+        def weave(h):
             nc.vector.tensor_copy(
-                out=woven[g, h][:].bitcast(I32).rearrange("p (n u) -> p n u", u=2),
-                in_=picked[g][:, :, HALF * h : HALF * (h + 1)].bitcast(I32).rearrange("p u n -> p n u"),
+                out=woven[1, h].bitcast(I32).rearrange("p (n u) -> p n u", u=2),
+                in_=picked[:, :, HALF * h : HALF * (h + 1)].bitcast(I32).rearrange("p u n -> p n u"),
             )
 
-        def quantize_x(g, h):
-            nc.vector.quantize_mx(out=x_words[g, h][:].bitcast(FP8X4), scales=x_bytes[g, h][:], in_=woven[g, h][:])
-
-        for h in range(2):
-            woven[0, h] = sb([P, HALF * PACK], BF16, f"woven0_{h}")
-            x_words[0, h] = sb([P, HALF], U32, f"x_words0_{h}")
-        for u in range(2):
-            cast_pair(0, u)
-            gather(0, u, 0, S)
-        for h in range(2):
-            weave(0, h)
-        for h in range(2):
-            quantize_x(0, h)
-        cast_pair(1, 0)
-        gather(1, 0, 0, S)
-        cast_pair(1, 1)
-        for h in range(2):
-            gather(1, 1, HALF * h, HALF * (h + 1))
-
-        w_grouped = {(g, q): at(8192 * g + 4096 * q, [P, 2, P, PACK], BF16, f"w_grouped{g}_{q}") for g in range(PASSES) for q in range(2)}
-        w_words = [sb([P, H], U32, f"w_words{g}") for g in range(PASSES)]
-        w_bytes = [sb([P, H], U8, f"w_bytes{g}") for g in range(PASSES)]
+        def quantize_x(g, h, a, b):
+            nc.vector.quantize_mx(out=x_words[g, h][:, a:b].bitcast(FP8X4), scales=x_bytes[g, h][:, a:b], in_=woven[g, h][:, PACK * a : PACK * b])
 
         def cast_w(g, n, q, on_scalar):
             src = w_raw[g, n][:].rearrange("p j (m t) -> p m j t", t=PACK)
-            mw = W_LOAD // PACK
-            dst = w_grouped[g, q][:].rearrange("p t m j -> p m j t")
-            move(on_scalar, dst[:, mw * n : mw * (n + 1)], src[:, :, :, 2 * q : 2 * q + 2])
+            m0 = sum(W_LOADS[g][:n]) // PACK
+            dst = w_grouped[g, q].rearrange("p t m j -> p m j t")
+            move(on_scalar, dst[:, m0 : m0 + W_LOADS[g][n] // PACK], src[:, :, :, 2 * q : 2 * q + 2])
 
-        def quantize_w(g, q):
+        def quantize_w(g, t0, t1):
             nc.vector.quantize_mx(
-                out=w_words[g][:, 2 * P * q : 2 * P * (q + 1)].bitcast(FP8X4),
-                scales=w_bytes[g][:, 2 * P * q : 2 * P * (q + 1)],
-                in_=w_grouped[g, q][:].rearrange("p t m j -> p (t m j)"),
+                out=w_words[g][:, P * t0 : P * t1].bitcast(FP8X4),
+                scales=w_bytes[g][:, P * t0 : P * t1],
+                in_=w_grouped[g, t0 // 2][:, t0 % 2 : t0 % 2 + t1 - t0].rearrange("p t m j -> p (t m j)"),
             )
 
         banks = {}
@@ -147,24 +157,61 @@ def tile_picked_deepset_none_e_kernel(tc, xT, w1, w2_words, w2_scales, offs, out
         def first_product(g, t, h):
             if g == 0:
                 banks[t, h] = psum.tile([P, HALF], F32, name=f"h{t}_{h}", tag=f"bank{2 * t + h}")
-            nc.tensor.matmul_mx(
-                out=banks[t, h][:],
-                lhsT=w_words[g][:, P * t : P * (t + 1)].bitcast(FP8X4),
-                lhsT_scale=w_bytes[g][:, P * t : P * (t + 1)],
-                rhs=x_words[g, h][:].bitcast(FP8X4),
-                rhs_scale=x_bytes[g, h][:],
-                start=(g == 0),
-                stop=(g == PASSES - 1),
-            )
+            cuts = (0, Q, HALF - LATE) if (g, h) == (0, 1) else (0, HALF)
+            parts = [(a, b, x_words[g, h][:, a:b], x_bytes[g, h][:, a:b]) for a, b in zip(cuts, cuts[1:])]
+            if (g, h) == (0, 1):
+                parts.append((HALF - LATE, HALF, late_words[:], late_bytes[:]))
+            for a, b, words, plane in parts:
+                nc.tensor.matmul_mx(
+                    out=banks[t, h][:, a:b],
+                    lhsT=w_words[g][:, P * t : P * (t + 1)].bitcast(FP8X4),
+                    lhsT_scale=w_bytes[g][:, P * t : P * (t + 1)],
+                    rhs=words.bitcast(FP8X4),
+                    rhs_scale=plane,
+                    start=(g == 0 and a == 0),
+                    stop=(g == PASSES - 1 and b == HALF),
+                )
 
-        cast_w(0, 0, 0, True)
-        cast_w(0, 0, 1, True)
-        cast_w(0, 1, 0, True)
-        cast_w(0, 1, 1, True)
-        for q in range(2):
-            quantize_w(0, q)
-            woven[1, q] = at(4096 * q, [P, HALF * PACK], BF16, f"woven1_{q}")
-            weave(1, q)
+        cast_pair(0, 0)
+        gather(0, 0, 0, S)
+        cast_pair(0, 1)
+        for h in range(2):
+            gather(0, 1, HALF * h, HALF * (h + 1))
+        for h in range(2):
+            x_words[0, h] = sb([P, HALF], U32, f"x_words0_{h}")
+        quantize_x(0, 0, 0, HALF)
+        quantize_x(0, 1, 0, Q)
+        quantize_x(0, 1, Q, HALF - LATE)
+        cast_pair(1, 0)
+        gather(1, 0, 0, S)
+        cast_pair(1, 1)
+        gather(1, 1, 0, Q)
+        late_words = at(0, [P, LATE], U32, "late_words")
+        late_bytes = sb([P, LATE], U8, "late_bytes")
+        nc.vector.quantize_mx(out=late_words[:].bitcast(FP8X4), scales=late_bytes[:], in_=woven[0, 1][:, PACK * (HALF - LATE) :])
+        gather(1, 1, Q, S)
+        if WARM:
+            warm = psum.tile([P, HALF], F32, name="warm", tag="bank7")
+        for n in range(WARM):
+            nc.tensor.matmul_mx(
+                out=warm[:],
+                lhsT=late_words[:].bitcast(FP8X4),
+                lhsT_scale=late_bytes[:],
+                rhs=x_words[0, 0][:].bitcast(FP8X4),
+                rhs_scale=x_bytes[0, 0][:],
+                start=True,
+                stop=True,
+            )
+        for n in range(2):
+            for q in range(2):
+                cast_w(0, n, q, True)
+        quantize_w(0, 0, 1)
+        quantize_w(0, 1, 2)
+        woven[1, 0] = area[:, 0 : HALF * PACK]
+        weave(0)
+        quantize_w(0, 2, 4)
+        woven[1, 1] = at(4096, [P, HALF * PACK], BF16, "woven1_1")[:]
+        weave(1)
         for t in range(PACK):
             for h in range(2):
                 first_product(0, t, h)
@@ -172,37 +219,34 @@ def tile_picked_deepset_none_e_kernel(tc, xT, w1, w2_words, w2_scales, offs, out
             for q in range(2):
                 cast_w(1, n, q, True)
         x_words[1, 0] = sb([P, HALF], U32, "x_words1_0")
-        quantize_x(1, 0)
-        quantize_w(1, 0)
+        quantize_x(1, 0, 0, HALF)
+        quantize_w(1, 0, 1)
+        quantize_w(1, 1, 2)
+        quantize_w(1, 2, 4)
         x_words[1, 1] = at(8192, [P, HALF], U32, "x_words1_1")
-        quantize_x(1, 1)
-        quantize_w(1, 1)
-        for q in range(2):
-            for h in range(2):
-                for t in range(2 * q, 2 * q + 2):
-                    first_product(1, t, h)
+        quantize_x(1, 1, 0, HALF)
+        for h in range(2):
+            for t in range(PACK):
+                first_product(1, t, h)
 
         h_sb = [sb([P, PACK, HALF], F32, f"h_sb{h}") for h in range(2)]
         sums = [sb([P, PACK], F32, f"sums{h}") for h in range(2)]
         neg_mean = sb([P, 1, PACK, 1], F32, "neg_mean")
-        for t in range(PACK):
-            nc.scalar.activation(out=h_sb[0][:, t, :], in_=banks[t, 0][:], func=ACT.Copy, accum_out=sums[0][:, t : t + 1])
-        for t in range(PACK):
-            if t < PACK - 1:
-                nc.vector.tensor_scalar(
-                    out=h_sb[1][:, t, :], in0=banks[t, 1][:], scalar1=-1.0 / S, scalar2=None,
-                    op0=ALU.mult, op1=ALU.add, accum_out=sums[1][:, t : t + 1],
-                )
-            else:
-                nc.scalar.activation(
-                    out=h_sb[1][:, t, :], in_=banks[t, 1][:], func=ACT.Copy, scale=-1.0 / S, accum_out=sums[1][:, t : t + 1]
-                )
-            if t >= PACK - 2:
-                t0 = 0 if t == PACK - 2 else t
-                nc.vector.scalar_tensor_tensor(
-                    out=neg_mean[:, 0, t0 : t + 1, 0], in0=sums[0][:, t0 : t + 1], scalar=-1.0 / S, in1=sums[1][:, t0 : t + 1],
-                    op0=ALU.mult, op1=ALU.add,
-                )
+        for h in range(2):
+            scale = 1.0 if h == 0 else -1.0 / S
+            for t in range(PACK):
+                if (t, h) in ON_VECTOR:
+                    nc.vector.tensor_scalar(
+                        out=h_sb[h][:, t, :], in0=banks[t, h][:], scalar1=scale, scalar2=None,
+                        op0=ALU.mult, op1=ALU.add, accum_out=sums[h][:, t : t + 1],
+                    )
+                else:
+                    nc.scalar.activation(out=h_sb[h][:, t, :], in_=banks[t, h][:], func=ACT.Copy, scale=scale, accum_out=sums[h][:, t : t + 1])
+        for t0 in (0, 2):
+            nc.vector.scalar_tensor_tensor(
+                out=neg_mean[:, 0, t0 : t0 + 2, 0], in0=sums[0][:, t0 : t0 + 2], scalar=-1.0 / S, in1=sums[1][:, t0 : t0 + 2],
+                op0=ALU.mult, op1=ALU.add,
+            )
 
         z_grouped = {}
         z_planes = {}
@@ -227,11 +271,13 @@ def tile_picked_deepset_none_e_kernel(tc, xT, w1, w2_words, w2_scales, offs, out
                     op=ALU.add,
                 )
 
-        def lay(n):
-            nc.vector.tensor_copy(
-                out=z_grouped[n][:].rearrange("p (c i) j -> p c j i", i=RUN),
-                in_=z_planes[n][:].rearrange("p j (c i) -> p c j i", i=RUN),
-            )
+        def lay(n, on_scalar):
+            dst = z_grouped[n][:].rearrange("p (c i) j -> p c j i", i=RUN)
+            src = z_planes[n][:].rearrange("p j (c i) -> p c j i", i=RUN)
+            if on_scalar:
+                nc.scalar.copy(out=dst, in_=src)
+            else:
+                nc.vector.tensor_copy(out=dst, in_=src)
 
         def second_product(n):
             c0, width, on_scalar = Z_CHUNKS[n]
@@ -251,17 +297,15 @@ def tile_picked_deepset_none_e_kernel(tc, xT, w1, w2_words, w2_scales, offs, out
                 stop=True,
             )
             staged = sb([P, width], F32, f"staged{n}")
-            move(True, staged[:], result[:, 0:width])
+            move(n != 1, staged[:], result[:, 0:width])
             queue = nc.scalar if n == len(Z_CHUNKS) - 1 else nc.sync
             queue.dma_start(out=out[:, c0 : c0 + width], in_=staged[:])
 
         for n in range(len(Z_CHUNKS)):
             subtract(n)
+        lay(4, True)
         second_product(0)
-        lay(2)
-        lay(3)
-        second_product(2)
-        second_product(3)
-        lay(4)
-        second_product(1)
-        second_product(4)
+        lay(2, False)
+        lay(3, False)
+        for n in (2, 3, 1, 4):
+            second_product(n)

@@ -24,10 +24,11 @@ HALF = 512
 RUN = 4
 LATE = 128
 Q = 256
-ON_VECTOR = ((3, 0), (0, 1), (2, 1))
-WARM = 2
+FIRST = 384
+ON_VECTOR = ((1, 0), (3, 0), (0, 1), (2, 1))
+WARM = 3
 
-X_CHUNKS = [[(1024, 0), (1024, 320)], [(1024, 1024), (1024, 352)], [(1024, 1024), (1024, 704)], [(768, 768), (768, 512), (512, 160)]]
+X_CHUNKS = [[(1024, 0), (1024, 320)], [(1024, 1024), (1024, 448)], [(1024, 1024), (1024, 768)], [(768, 768), (768, 512), (512, 224)]]
 W_LOADS = [[256, 256], [256, 256]]
 Z_CHUNKS = [(0, 256, False), (256, 128, False), (512, 256, True), (768, 256, True), (384, 128, True)]
 
@@ -157,7 +158,7 @@ def tile_picked_deepset_none_e_kernel(tc, xT, w1, w2_words, w2_scales, offs, out
         def first_product(g, t, h):
             if g == 0:
                 banks[t, h] = psum.tile([P, HALF], F32, name=f"h{t}_{h}", tag=f"bank{2 * t + h}")
-            cuts = (0, Q, HALF - LATE) if (g, h) == (0, 1) else (0, HALF)
+            cuts = {(0, 1): (0, Q, HALF - LATE), (1, 1): (0, Q, HALF)}.get((g, h), (0, HALF))
             parts = [(a, b, x_words[g, h][:, a:b], x_bytes[g, h][:, a:b]) for a, b in zip(cuts, cuts[1:])]
             if (g, h) == (0, 1):
                 parts.append((HALF - LATE, HALF, late_words[:], late_bytes[:]))
@@ -185,11 +186,11 @@ def tile_picked_deepset_none_e_kernel(tc, xT, w1, w2_words, w2_scales, offs, out
         cast_pair(1, 0)
         gather(1, 0, 0, S)
         cast_pair(1, 1)
-        gather(1, 1, 0, Q)
+        gather(1, 1, 0, FIRST)
         late_words = at(0, [P, LATE], U32, "late_words")
         late_bytes = sb([P, LATE], U8, "late_bytes")
         nc.vector.quantize_mx(out=late_words[:].bitcast(FP8X4), scales=late_bytes[:], in_=woven[0, 1][:, PACK * (HALF - LATE) :])
-        gather(1, 1, Q, S)
+        gather(1, 1, FIRST, S)
         if WARM:
             warm = psum.tile([P, HALF], F32, name="warm", tag="bank7")
         for n in range(WARM):
@@ -224,7 +225,8 @@ def tile_picked_deepset_none_e_kernel(tc, xT, w1, w2_words, w2_scales, offs, out
         quantize_w(1, 1, 2)
         quantize_w(1, 2, 4)
         x_words[1, 1] = at(8192, [P, HALF], U32, "x_words1_1")
-        quantize_x(1, 1, 0, HALF)
+        quantize_x(1, 1, 0, Q)
+        quantize_x(1, 1, Q, HALF)
         for h in range(2):
             for t in range(PACK):
                 first_product(1, t, h)

@@ -21,15 +21,10 @@ PACK = 4
 K_PASS = P * PACK
 PASSES = K // K_PASS
 HALF = 512
-RUN = 4
-LATE = 128
 Q = 256
-FIRST = 384
+RUN = 4
 ON_VECTOR = ((1, 0), (3, 0), (0, 1), (2, 1))
-WARM = 3
-
-X_CHUNKS = [[(1024, 0), (1024, 320)], [(1024, 1024), (1024, 448)], [(1024, 1024), (1024, 768)], [(768, 768), (768, 512), (512, 224)]]
-W_LOADS = [[256, 256], [256, 256]]
+W_ON_VECTOR = (80, 88)
 Z_CHUNKS = [(0, 256, False), (256, 128, False), (512, 256, True), (768, 256, True), (384, 128, True)]
 
 
@@ -54,37 +49,24 @@ def tile_picked_deepset_none_e_kernel(tc, xT, w1, w2_words, w2_scales, offs, out
         x_raw = {}
         w_raw = {}
 
-        def load_pair(g, u):
+        def load_x(g, j):
             rows = xT[g * K_PASS : (g + 1) * K_PASS, :].rearrange("(p j) w -> p j w", j=PACK)
-            c0 = 0
-            for n, (width, on_scalar) in enumerate(X_CHUNKS[2 * g + u]):
-                if (g, u, n) == (1, 1, len(X_CHUNKS[3]) - 1):
-                    raw = at(0, [P, 2, width], F32, "x_raw_last")
-                else:
-                    raw = sb([P, 2, width], F32, f"x_raw{g}_{u}_{n}")
-                nc.sync.dma_start(out=raw[:], in_=rows[:, 2 * u : 2 * u + 2, c0 : c0 + width])
-                x_raw[g, u, n] = raw
-                if (g, u, n) == (0, 0, 0):
-                    nc.sync.dma_start(offsets[:], offs)
-                c0 = c0 + width
+            x_raw[g, j] = sb([P, T], F32, f"x_raw{g}_{j}")
+            nc.sync.dma_start(out=x_raw[g, j][:], in_=rows[:, j, :])
 
         def load_w(g):
-            c0 = 0
-            for n, width in enumerate(W_LOADS[g]):
-                if n == 1:
-                    raw = at(4096 + 4096 * g, [P, PACK, width], F32, f"w_raw{g}_{n}")
-                else:
-                    raw = sb([P, PACK, width], F32, f"w_raw{g}_{n}")
-                rows = w1[g * K_PASS : (g + 1) * K_PASS, c0 : c0 + width]
-                nc.sync.dma_start(out=raw[:], in_=rows.rearrange("(p j) w -> p j w", j=PACK))
-                w_raw[g, n] = raw
-                c0 = c0 + width
+            rows = w1[g * K_PASS : (g + 1) * K_PASS, :].rearrange("(p j) w -> p (j w)", j=PACK)
+            w_raw[g] = at(8192 * g, [P, PACK * H], F32, f"w_raw{g}")
+            nc.sync.dma_start(out=w_raw[g][:], in_=rows)
 
-        load_pair(0, 0)
-        load_pair(0, 1)
-        load_pair(1, 0)
-        load_pair(1, 1)
+        load_x(0, 0)
+        nc.sync.dma_start(offsets[:], offs)
+        for j in range(1, PACK):
+            load_x(0, j)
+        for j in range(PACK - 1):
+            load_x(1, j)
         load_w(0)
+        load_x(1, PACK - 1)
         load_w(1)
         nc.sync.dma_start(out=w2_codes[:].bitcast(I32), in_=w2_words[0].bitcast(I32))
         for q in range(4):
@@ -99,58 +81,52 @@ def tile_picked_deepset_none_e_kernel(tc, xT, w1, w2_words, w2_scales, offs, out
             else:
                 nc.vector.tensor_copy(out=dst, in_=src)
 
-        x_pairs = {}
-        direct = sb([P, S * PACK], BF16, "direct")
-        picked = sb([P, 2, S], U32, "picked")
-        woven = {(0, h): direct[:, PACK * HALF * h : PACK * HALF * (h + 1)] for h in range(2)}
+        def move16(on_scalar, dst, src):
+            if on_scalar:
+                nc.scalar.copy(out=dst, in_=src)
+            else:
+                nc.vector.tensor_copy(out=dst, in_=src)
+
+        planes = {(g, h): sb([P, PACK - g, HALF], BF16, f"planes{g}_{h}") for g in range(PASSES) for h in range(2)}
+        woven = {(g, h): sb([P, HALF * PACK], BF16, f"woven{g}_{h}") for g in range(PASSES) for h in range(2)}
         x_words = {}
         x_bytes = {(g, h): sb([P, HALF], U8, f"x_bytes{g}_{h}") for g in range(PASSES) for h in range(2)}
-        area = sb([P, (HALF + P) * PACK], BF16, "area")
-        w_grouped = {(g, q): sb([P, 2, P, PACK], BF16, f"w_grouped{g}_{q}")[:] for g in range(PASSES) for q in range(2) if (g, q) != (0, 0)}
-        w_grouped[0, 0] = area[:, (HALF - P) * PACK :].rearrange("p (t m j) -> p t m j", t=2, j=PACK)
+        w_grouped = [sb([P, PACK, P, PACK], BF16, f"w_grouped{g}") for g in range(PASSES)]
         w_words = [sb([P, H], U32, f"w_words{g}") for g in range(PASSES)]
         w_bytes = [sb([P, H], U8, f"w_bytes{g}") for g in range(PASSES)]
 
-        def cast_pair(g, u):
-            pairs = sb([P, T, 2], BF16, f"x_pairs{g}_{u}")
-            x_pairs[g, u] = pairs
-            c0 = 0
-            for n, (width, on_scalar) in enumerate(X_CHUNKS[2 * g + u]):
-                src = x_raw[g, u, n][:].rearrange("p e w -> p w e")
-                if on_scalar > 0:
-                    move(True, pairs[:, c0 : c0 + on_scalar, :], src[:, 0:on_scalar, :])
-                if on_scalar < width:
-                    move(False, pairs[:, c0 + on_scalar : c0 + width, :], src[:, on_scalar:width, :])
-                c0 = c0 + width
+        def gather(on_scalar, g, j, dst, a, b):
+            move(on_scalar, dst, x_raw[g, j][:].indirect(offsets[:, a // 16 : b // 16]))
 
-        def gather(g, u, a, b):
-            window = x_pairs[g, u][:].rearrange("p w e -> p (w e)").bitcast(U32)
-            if g == 0:
-                dst = direct[:].bitcast(U32).rearrange("p (n u) -> p n u", u=2)[:, a:b, u]
-            else:
-                dst = picked[:, u, a:b]
-            nc.vector.tensor_copy(dst, window.indirect(offsets[:, a // 16 : b // 16]))
+        def gather_plane(g, j, on_scalar):
+            for h in range(2):
+                gather(on_scalar[h], g, j, planes[g, h][:, j, :], HALF * h, HALF * (h + 1))
 
-        def weave(h):
-            nc.vector.tensor_copy(
-                out=woven[1, h].bitcast(I32).rearrange("p (n u) -> p n u", u=2),
-                in_=picked[:, :, HALF * h : HALF * (h + 1)].bitcast(I32).rearrange("p u n -> p n u"),
-            )
+        def lay_planes(on_scalar, g, h, a, b):
+            rows = PACK - g
+            dst = woven[g, h][:, PACK * a : PACK * b].rearrange("p (c i t) -> p c t i", i=RUN, t=PACK)[:, :, 0:rows, :]
+            src = planes[g, h][:, :, a:b].rearrange("p t (c i) -> p c t i", i=RUN)
+            move16(on_scalar, dst, src)
 
-        def quantize_x(g, h, a, b):
-            nc.vector.quantize_mx(out=x_words[g, h][:, a:b].bitcast(FP8X4), scales=x_bytes[g, h][:, a:b], in_=woven[g, h][:, PACK * a : PACK * b])
+        def last_slot(q):
+            h, a = divmod(Q * q, HALF)
+            return woven[1, h][:].rearrange("p (c t) -> p c t", t=PACK)[:, a : a + Q, PACK - 1]
 
-        def cast_w(g, n, q, on_scalar):
-            src = w_raw[g, n][:].rearrange("p j (m t) -> p m j t", t=PACK)
-            m0 = sum(W_LOADS[g][:n]) // PACK
-            dst = w_grouped[g, q].rearrange("p t m j -> p m j t")
-            move(on_scalar, dst[:, m0 : m0 + W_LOADS[g][n] // PACK], src[:, :, :, 2 * q : 2 * q + 2])
+        def quantize_x(g, h):
+            nc.vector.quantize_mx(out=x_words[g, h][:].bitcast(FP8X4), scales=x_bytes[g, h][:], in_=woven[g, h][:])
+
+        def cast_w(g):
+            src = w_raw[g][:].rearrange("p (j m t) -> p m j t", j=PACK, t=PACK)
+            dst = w_grouped[g][:].rearrange("p t m j -> p m j t")
+            cut = W_ON_VECTOR[g]
+            move(False, dst[:, 0:cut], src[:, 0:cut])
+            move(True, dst[:, cut:P], src[:, cut:P])
 
         def quantize_w(g, t0, t1):
             nc.vector.quantize_mx(
                 out=w_words[g][:, P * t0 : P * t1].bitcast(FP8X4),
                 scales=w_bytes[g][:, P * t0 : P * t1],
-                in_=w_grouped[g, t0 // 2][:, t0 % 2 : t0 % 2 + t1 - t0].rearrange("p t m j -> p (t m j)"),
+                in_=w_grouped[g][:, t0:t1].rearrange("p t m j -> p (t m j)"),
             )
 
         banks = {}
@@ -158,75 +134,51 @@ def tile_picked_deepset_none_e_kernel(tc, xT, w1, w2_words, w2_scales, offs, out
         def first_product(g, t, h):
             if g == 0:
                 banks[t, h] = psum.tile([P, HALF], F32, name=f"h{t}_{h}", tag=f"bank{2 * t + h}")
-            cuts = {(0, 1): (0, Q, HALF - LATE), (1, 1): (0, Q, HALF)}.get((g, h), (0, HALF))
-            parts = [(a, b, x_words[g, h][:, a:b], x_bytes[g, h][:, a:b]) for a, b in zip(cuts, cuts[1:])]
-            if (g, h) == (0, 1):
-                parts.append((HALF - LATE, HALF, late_words[:], late_bytes[:]))
-            for a, b, words, plane in parts:
-                nc.tensor.matmul_mx(
-                    out=banks[t, h][:, a:b],
-                    lhsT=w_words[g][:, P * t : P * (t + 1)].bitcast(FP8X4),
-                    lhsT_scale=w_bytes[g][:, P * t : P * (t + 1)],
-                    rhs=words.bitcast(FP8X4),
-                    rhs_scale=plane,
-                    start=(g == 0 and a == 0),
-                    stop=(g == PASSES - 1 and b == HALF),
-                )
+            nc.tensor.matmul_mx(
+                out=banks[t, h][:],
+                lhsT=w_words[g][:, P * t : P * (t + 1)].bitcast(FP8X4),
+                lhsT_scale=w_bytes[g][:, P * t : P * (t + 1)],
+                rhs=x_words[g, h][:].bitcast(FP8X4),
+                rhs_scale=x_bytes[g, h][:],
+                start=(g == 0),
+                stop=(g == PASSES - 1),
+            )
 
-        cast_pair(0, 0)
-        gather(0, 0, 0, S)
-        cast_pair(0, 1)
+        for j in range(PACK):
+            gather_plane(0, j, (False, True))
         for h in range(2):
-            gather(0, 1, HALF * h, HALF * (h + 1))
+            lay_planes(False, 0, h, 0, HALF)
         for h in range(2):
             x_words[0, h] = sb([P, HALF], U32, f"x_words0_{h}")
-        quantize_x(0, 0, 0, HALF)
-        quantize_x(0, 1, 0, Q)
-        quantize_x(0, 1, Q, HALF - LATE)
-        cast_pair(1, 0)
-        gather(1, 0, 0, S)
-        cast_pair(1, 1)
-        gather(1, 1, 0, FIRST)
-        late_words = at(0, [P, LATE], U32, "late_words")
-        late_bytes = sb([P, LATE], U8, "late_bytes")
-        nc.vector.quantize_mx(out=late_words[:].bitcast(FP8X4), scales=late_bytes[:], in_=woven[0, 1][:, PACK * (HALF - LATE) :])
-        gather(1, 1, FIRST, S)
-        if WARM:
-            warm = psum.tile([P, HALF], F32, name="warm", tag="bank7")
-        for n in range(WARM):
-            nc.tensor.matmul_mx(
-                out=warm[:],
-                lhsT=late_words[:].bitcast(FP8X4),
-                lhsT_scale=late_bytes[:],
-                rhs=x_words[0, 0][:].bitcast(FP8X4),
-                rhs_scale=x_bytes[0, 0][:],
-                start=True,
-                stop=True,
-            )
-        for n in range(2):
-            for q in range(2):
-                cast_w(0, n, q, True)
-        quantize_w(0, 0, 1)
-        quantize_w(0, 1, 2)
-        woven[1, 0] = area[:, 0 : HALF * PACK]
-        weave(0)
+            quantize_x(0, h)
+        gather_plane(1, 0, (True, True))
+        gather_plane(1, 1, (False, True))
+        gather_plane(1, 2, (False, True))
+        lay_planes(False, 1, 0, 0, HALF)
+        lay_planes(False, 1, 1, 0, Q)
+        lay_planes(True, 1, 1, Q, HALF)
+        cast_w(0)
+        quantize_w(0, 0, 2)
         quantize_w(0, 2, 4)
-        woven[1, 1] = at(4096, [P, HALF * PACK], BF16, "woven1_1")[:]
-        weave(1)
         for t in range(PACK):
             for h in range(2):
                 first_product(0, t, h)
-        for n in range(2):
-            for q in range(2):
-                cast_w(1, n, q, True)
+
+        gather(False, 1, PACK - 1, last_slot(0), 0, Q)
+        last = {q: sb([P, Q], BF16, f"last{q}") for q in range(1, 4)}
+        for q in range(1, 4):
+            gather(True, 1, PACK - 1, last[q][:], Q * q, Q * (q + 1))
+        move16(False, last_slot(1), last[1][:])
         x_words[1, 0] = sb([P, HALF], U32, "x_words1_0")
-        quantize_x(1, 0, 0, HALF)
+        move16(False, last_slot(2), last[2][:])
+        quantize_x(1, 0)
+        move16(True, last_slot(3), last[3][:])
+        cast_w(1)
         quantize_w(1, 0, 1)
         quantize_w(1, 1, 2)
         quantize_w(1, 2, 4)
         x_words[1, 1] = at(8192, [P, HALF], U32, "x_words1_1")
-        quantize_x(1, 1, 0, Q)
-        quantize_x(1, 1, Q, HALF)
+        quantize_x(1, 1)
         for h in range(2):
             for t in range(PACK):
                 first_product(1, t, h)

@@ -23,8 +23,9 @@ PASSES = K // K_PASS
 HALF = 512
 Q = 256
 RUN = 4
-ON_VECTOR = ((1, 0), (3, 0), (0, 1), (2, 1))
-W_ON_VECTOR = (80, 88)
+LATE = 128
+ON_VECTOR = ((2, 0), (3, 0), (2, 1))
+W_ON_VECTOR = (80, 84)
 Z_CHUNKS = [(0, 256, False), (256, 128, False), (512, 256, True), (768, 256, True), (384, 128, True)]
 
 
@@ -108,19 +109,19 @@ def tile_picked_deepset_none_e_kernel(tc, xT, w1, w2_words, w2_scales, offs, out
             src = planes[g, h][:, :, a:b].rearrange("p t (c i) -> p c t i", i=RUN)
             move16(on_scalar, dst, src)
 
-        def last_slot(q):
-            h, a = divmod(Q * q, HALF)
-            return woven[1, h][:].rearrange("p (c t) -> p c t", t=PACK)[:, a : a + Q, PACK - 1]
+        def last_slot(a, b):
+            h = a // HALF
+            return woven[1, h][:].rearrange("p (c t) -> p c t", t=PACK)[:, a - HALF * h : b - HALF * h, PACK - 1]
 
         def quantize_x(g, h):
             nc.vector.quantize_mx(out=x_words[g, h][:].bitcast(FP8X4), scales=x_bytes[g, h][:], in_=woven[g, h][:])
 
-        def cast_w(g):
+        def cast_w(g, t0, t1):
             src = w_raw[g][:].rearrange("p (j m t) -> p m j t", j=PACK, t=PACK)
             dst = w_grouped[g][:].rearrange("p t m j -> p m j t")
             cut = W_ON_VECTOR[g]
-            move(False, dst[:, 0:cut], src[:, 0:cut])
-            move(True, dst[:, cut:P], src[:, cut:P])
+            move(False, dst[:, 0:cut, :, t0:t1], src[:, 0:cut, :, t0:t1])
+            move(True, dst[:, cut:P, :, t0:t1], src[:, cut:P, :, t0:t1])
 
         def quantize_w(g, t0, t1):
             nc.vector.quantize_mx(
@@ -155,25 +156,27 @@ def tile_picked_deepset_none_e_kernel(tc, xT, w1, w2_words, w2_scales, offs, out
         gather_plane(1, 1, (False, True))
         gather_plane(1, 2, (False, True))
         lay_planes(False, 1, 0, 0, HALF)
-        lay_planes(False, 1, 1, 0, Q)
-        lay_planes(True, 1, 1, Q, HALF)
-        cast_w(0)
+        lay_planes(False, 1, 1, 0, HALF - LATE)
+        lay_planes(True, 1, 1, HALF - LATE, HALF)
+        cast_w(0, 0, 4)
         quantize_w(0, 0, 2)
         quantize_w(0, 2, 4)
         for t in range(PACK):
             for h in range(2):
                 first_product(0, t, h)
 
-        gather(False, 1, PACK - 1, last_slot(0), 0, Q)
-        last = {q: sb([P, Q], BF16, f"last{q}") for q in range(1, 4)}
-        for q in range(1, 4):
-            gather(True, 1, PACK - 1, last[q][:], Q * q, Q * (q + 1))
-        move16(False, last_slot(1), last[1][:])
+        gather(False, 1, PACK - 1, last_slot(0, Q), 0, Q)
+        last = {a: sb([P, Q], BF16, f"last{a}") for a in range(Q, S, Q)}
+        for a in range(Q, S, Q):
+            gather(True, 1, PACK - 1, last[a][:], a, a + Q)
+        move16(False, last_slot(Q, HALF), last[Q][:])
         x_words[1, 0] = sb([P, HALF], U32, "x_words1_0")
-        move16(False, last_slot(2), last[2][:])
+        move16(False, last_slot(HALF, HALF + Q), last[HALF][:])
         quantize_x(1, 0)
-        move16(True, last_slot(3), last[3][:])
-        cast_w(1)
+        move16(False, last_slot(HALF + Q, S - LATE), last[HALF + Q][:, 0 : Q - LATE])
+        move16(True, last_slot(S - LATE, S), last[HALF + Q][:, Q - LATE : Q])
+        cast_w(1, 0, 2)
+        cast_w(1, 2, 4)
         quantize_w(1, 0, 1)
         quantize_w(1, 1, 2)
         quantize_w(1, 2, 4)
@@ -196,14 +199,20 @@ def tile_picked_deepset_none_e_kernel(tc, xT, w1, w2_words, w2_scales, offs, out
                     )
                 else:
                     nc.scalar.activation(out=h_sb[h][:, t, :], in_=banks[t, h][:], func=ACT.Copy, scale=scale, accum_out=sums[h][:, t : t + 1])
+        z_grouped = {}
+        z_planes = {n: sb([P, PACK, width], BF16, f"z_planes{n}") for n, (c0, width, on_scalar) in enumerate(Z_CHUNKS) if on_scalar}
+        early = ((2, 0), (2, 1))
         for t0 in (0, 2):
             nc.vector.scalar_tensor_tensor(
                 out=neg_mean[:, 0, t0 : t0 + 2, 0], in0=sums[0][:, t0 : t0 + 2], scalar=-1.0 / S, in1=sums[1][:, t0 : t0 + 2],
                 op0=ALU.mult, op1=ALU.add,
             )
-
-        z_grouped = {}
-        z_planes = {}
+            n, t = early[t0 // 2]
+            c0, width, on_scalar = Z_CHUNKS[n]
+            nc.vector.tensor_scalar(
+                out=z_planes[n][:, t, :], in0=h_sb[1][:, t, c0 - HALF : c0 - HALF + width], scalar1=-float(S), scalar2=neg_mean[:, 0, t, :],
+                op0=ALU.mult, op1=ALU.add,
+            )
 
         def source(n):
             c0, width, on_scalar = Z_CHUNKS[n]
@@ -214,9 +223,9 @@ def tile_picked_deepset_none_e_kernel(tc, xT, w1, w2_words, w2_scales, offs, out
             src = source(n)
             z_grouped[n] = sb([P, width, PACK], BF16, f"z_grouped{n}")
             if on_scalar:
-                z_planes[n] = sb([P, PACK, width], BF16, f"z_planes{n}")
                 for t in range(PACK):
-                    nc.scalar.activation(out=z_planes[n][:, t, :], in_=src[:, t, :], func=ACT.Identity, bias=neg_mean[:, 0, t, :], scale=(1.0 if c0 < HALF else -float(S)))
+                    if (n, t) not in early:
+                        nc.scalar.activation(out=z_planes[n][:, t, :], in_=src[:, t, :], func=ACT.Identity, bias=neg_mean[:, 0, t, :], scale=(1.0 if c0 < HALF else -float(S)))
             else:
                 nc.vector.tensor_tensor(
                     out=z_grouped[n][:].rearrange("p (c i) t -> p c t i", i=RUN),
@@ -225,9 +234,9 @@ def tile_picked_deepset_none_e_kernel(tc, xT, w1, w2_words, w2_scales, offs, out
                     op=ALU.add,
                 )
 
-        def lay(n, on_scalar):
-            dst = z_grouped[n][:].rearrange("p (c i) j -> p c j i", i=RUN)
-            src = z_planes[n][:].rearrange("p j (c i) -> p c j i", i=RUN)
+        def lay(n, on_scalar, a, b):
+            dst = z_grouped[n][:, a:b].rearrange("p (c i) j -> p c j i", i=RUN)
+            src = z_planes[n][:, :, a:b].rearrange("p j (c i) -> p c j i", i=RUN)
             if on_scalar:
                 nc.scalar.copy(out=dst, in_=src)
             else:
@@ -257,9 +266,10 @@ def tile_picked_deepset_none_e_kernel(tc, xT, w1, w2_words, w2_scales, offs, out
 
         for n in range(len(Z_CHUNKS)):
             subtract(n)
-        lay(4, True)
+        lay(3, True, 128, 256)
+        lay(4, True, 0, 128)
         second_product(0)
-        lay(2, False)
-        lay(3, False)
+        lay(2, False, 0, 256)
+        lay(3, False, 0, 128)
         for n in (2, 3, 1, 4):
             second_product(n)

@@ -175,8 +175,7 @@ def tile_picked_deepset_none_e_kernel(tc, xT, w1, w2_words, w2_scales, offs, out
         quantize_x(1, 0)
         move16(False, last_slot(HALF + Q, S - LATE), last[HALF + Q][:, 0 : Q - LATE])
         move16(True, last_slot(S - LATE, S), last[HALF + Q][:, Q - LATE : Q])
-        cast_w(1, 0, 2)
-        cast_w(1, 2, 4)
+        cast_w(1, 0, 4)
         quantize_w(1, 0, 1)
         quantize_w(1, 1, 2)
         quantize_w(1, 2, 4)

@@ -24,8 +24,8 @@ HALF = 512
 Q = 256
 RUN = 4
 LATE = 128
-ON_VECTOR = ((2, 0), (3, 0), (2, 1))
-W_ON_VECTOR = (80, 84)
+ON_VECTOR = ((1, 0), (3, 0), (0, 1), (2, 1))
+W_ON_VECTOR = (84, 88)
 Z_CHUNKS = [(0, 256, False), (256, 128, False), (512, 256, True), (768, 256, True), (384, 128, True)]
 
 
@@ -156,8 +156,8 @@ def tile_picked_deepset_none_e_kernel(tc, xT, w1, w2_words, w2_scales, offs, out
         gather_plane(1, 1, (False, True))
         gather_plane(1, 2, (False, True))
         lay_planes(False, 1, 0, 0, HALF)
-        lay_planes(False, 1, 1, 0, HALF - LATE)
-        lay_planes(True, 1, 1, HALF - LATE, HALF)
+        lay_planes(False, 1, 1, 0, Q)
+        lay_planes(True, 1, 1, Q, HALF)
         cast_w(0, 0, 4)
         quantize_w(0, 0, 2)
         quantize_w(0, 2, 4)
@@ -265,10 +265,9 @@ def tile_picked_deepset_none_e_kernel(tc, xT, w1, w2_words, w2_scales, offs, out
 
         for n in range(len(Z_CHUNKS)):
             subtract(n)
-        lay(3, True, 128, 256)
         lay(4, True, 0, 128)
         second_product(0)
         lay(2, False, 0, 256)
-        lay(3, False, 0, 128)
+        lay(3, False, 0, 256)
         for n in (2, 3, 1, 4):
             second_product(n)

@@ -25,7 +25,7 @@ Q = 256
 RUN = 4
 LATE = 128
 ON_VECTOR = ((1, 0), (3, 0), (0, 1), (2, 1))
-W_ON_VECTOR = (84, 88)
+W_ON_VECTOR = (80, 88)
 Z_CHUNKS = [(0, 256, False), (256, 128, False), (512, 256, True), (768, 256, True), (384, 128, True)]
 
 
@@ -198,20 +198,14 @@ def tile_picked_deepset_none_e_kernel(tc, xT, w1, w2_words, w2_scales, offs, out
                     )
                 else:
                     nc.scalar.activation(out=h_sb[h][:, t, :], in_=banks[t, h][:], func=ACT.Copy, scale=scale, accum_out=sums[h][:, t : t + 1])
-        z_grouped = {}
-        z_planes = {n: sb([P, PACK, width], BF16, f"z_planes{n}") for n, (c0, width, on_scalar) in enumerate(Z_CHUNKS) if on_scalar}
-        early = ((2, 0), (2, 1))
         for t0 in (0, 2):
             nc.vector.scalar_tensor_tensor(
                 out=neg_mean[:, 0, t0 : t0 + 2, 0], in0=sums[0][:, t0 : t0 + 2], scalar=-1.0 / S, in1=sums[1][:, t0 : t0 + 2],
                 op0=ALU.mult, op1=ALU.add,
             )
-            n, t = early[t0 // 2]
-            c0, width, on_scalar = Z_CHUNKS[n]
-            nc.vector.tensor_scalar(
-                out=z_planes[n][:, t, :], in0=h_sb[1][:, t, c0 - HALF : c0 - HALF + width], scalar1=-float(S), scalar2=neg_mean[:, 0, t, :],
-                op0=ALU.mult, op1=ALU.add,
-            )
+
+        z_grouped = {}
+        z_planes = {}
 
         def source(n):
             c0, width, on_scalar = Z_CHUNKS[n]
@@ -222,9 +216,9 @@ def tile_picked_deepset_none_e_kernel(tc, xT, w1, w2_words, w2_scales, offs, out
             src = source(n)
             z_grouped[n] = sb([P, width, PACK], BF16, f"z_grouped{n}")
             if on_scalar:
+                z_planes[n] = sb([P, PACK, width], BF16, f"z_planes{n}")
                 for t in range(PACK):
-                    if (n, t) not in early:
-                        nc.scalar.activation(out=z_planes[n][:, t, :], in_=src[:, t, :], func=ACT.Identity, bias=neg_mean[:, 0, t, :], scale=(1.0 if c0 < HALF else -float(S)))
+                    nc.scalar.activation(out=z_planes[n][:, t, :], in_=src[:, t, :], func=ACT.Identity, bias=neg_mean[:, 0, t, :], scale=(1.0 if c0 < HALF else -float(S)))
             else:
                 nc.vector.tensor_tensor(
                     out=z_grouped[n][:].rearrange("p (c i) t -> p c t i", i=RUN),
@@ -233,9 +227,9 @@ def tile_picked_deepset_none_e_kernel(tc, xT, w1, w2_words, w2_scales, offs, out
                     op=ALU.add,
                 )
 
-        def lay(n, on_scalar, a, b):
-            dst = z_grouped[n][:, a:b].rearrange("p (c i) j -> p c j i", i=RUN)
-            src = z_planes[n][:, :, a:b].rearrange("p j (c i) -> p c j i", i=RUN)
+        def lay(n, on_scalar):
+            dst = z_grouped[n][:].rearrange("p (c i) j -> p c j i", i=RUN)
+            src = z_planes[n][:].rearrange("p j (c i) -> p c j i", i=RUN)
             if on_scalar:
                 nc.scalar.copy(out=dst, in_=src)
             else:
@@ -265,9 +259,9 @@ def tile_picked_deepset_none_e_kernel(tc, xT, w1, w2_words, w2_scales, offs, out
 
         for n in range(len(Z_CHUNKS)):
             subtract(n)
-        lay(4, True, 0, 128)
+        lay(4, True)
         second_product(0)
-        lay(2, False, 0, 256)
-        lay(3, False, 0, 256)
+        lay(2, False)
+        lay(3, False)
         for n in (2, 3, 1, 4):
             second_product(n)

@@ -25,7 +25,10 @@ Q = 256
 RUN = 4
 LATE = 128
 ON_VECTOR = ((1, 0), (3, 0), (0, 1), (2, 1))
-W_ON_VECTOR = (80, 88)
+HALF1_ORDER = (0, 3, 2, 1)
+FOLDED = (1, 2)
+RESULT_BANKS = (0, 2, 4, 6, 1)
+W_ON_VECTOR = (84, 92)
 Z_CHUNKS = [(0, 256, False), (256, 128, False), (512, 256, True), (768, 256, True), (384, 128, True)]
 
 
@@ -88,7 +91,7 @@ def tile_picked_deepset_none_e_kernel(tc, xT, w1, w2_words, w2_scales, offs, out
             else:
                 nc.vector.tensor_copy(out=dst, in_=src)
 
-        planes = {(g, h): sb([P, PACK - g, HALF], BF16, f"planes{g}_{h}") for g in range(PASSES) for h in range(2)}
+        planes = {(g, h): sb([P, PACK, HALF], BF16, f"planes{g}_{h}") for g in range(PASSES) for h in range(2)}
         woven = {(g, h): sb([P, HALF * PACK], BF16, f"woven{g}_{h}") for g in range(PASSES) for h in range(2)}
         x_words = {}
         x_bytes = {(g, h): sb([P, HALF], U8, f"x_bytes{g}_{h}") for g in range(PASSES) for h in range(2)}
@@ -106,7 +109,7 @@ def tile_picked_deepset_none_e_kernel(tc, xT, w1, w2_words, w2_scales, offs, out
         def lay_planes(on_scalar, g, h, a, b):
             rows = PACK - g
             dst = woven[g, h][:, PACK * a : PACK * b].rearrange("p (c i t) -> p c t i", i=RUN, t=PACK)[:, :, 0:rows, :]
-            src = planes[g, h][:, :, a:b].rearrange("p t (c i) -> p c t i", i=RUN)
+            src = planes[g, h][:, 0:rows, a:b].rearrange("p t (c i) -> p c t i", i=RUN)
             move16(on_scalar, dst, src)
 
         def last_slot(a, b):
@@ -116,12 +119,12 @@ def tile_picked_deepset_none_e_kernel(tc, xT, w1, w2_words, w2_scales, offs, out
         def quantize_x(g, h):
             nc.vector.quantize_mx(out=x_words[g, h][:].bitcast(FP8X4), scales=x_bytes[g, h][:], in_=woven[g, h][:])
 
-        def cast_w(g, t0, t1):
+        def cast_w(g):
             src = w_raw[g][:].rearrange("p (j m t) -> p m j t", j=PACK, t=PACK)
             dst = w_grouped[g][:].rearrange("p t m j -> p m j t")
             cut = W_ON_VECTOR[g]
-            move(False, dst[:, 0:cut, :, t0:t1], src[:, 0:cut, :, t0:t1])
-            move(True, dst[:, cut:P, :, t0:t1], src[:, cut:P, :, t0:t1])
+            move(False, dst[:, 0:cut], src[:, 0:cut])
+            move(True, dst[:, cut:P], src[:, cut:P])
 
         def quantize_w(g, t0, t1):
             nc.vector.quantize_mx(
@@ -156,53 +159,80 @@ def tile_picked_deepset_none_e_kernel(tc, xT, w1, w2_words, w2_scales, offs, out
         gather_plane(1, 1, (False, True))
         gather_plane(1, 2, (False, True))
         lay_planes(False, 1, 0, 0, HALF)
-        lay_planes(False, 1, 1, 0, Q)
-        lay_planes(True, 1, 1, Q, HALF)
-        cast_w(0, 0, 4)
+        lay_planes(False, 1, 1, 0, LATE)
+        lay_planes(True, 1, 1, LATE, HALF - LATE)
+        cast_w(0)
         quantize_w(0, 0, 2)
         quantize_w(0, 2, 4)
         for t in range(PACK):
             for h in range(2):
                 first_product(0, t, h)
 
+        def last_plane(a, b):
+            h = a // HALF
+            return planes[1, h][:, PACK - 1, a - HALF * h : b - HALF * h]
+
         gather(False, 1, PACK - 1, last_slot(0, Q), 0, Q)
-        last = {a: sb([P, Q], BF16, f"last{a}") for a in range(Q, S, Q)}
         for a in range(Q, S, Q):
-            gather(True, 1, PACK - 1, last[a][:], a, a + Q)
-        move16(False, last_slot(Q, HALF), last[Q][:])
+            gather(True, 1, PACK - 1, last_plane(a, a + Q), a, a + Q)
+        move16(False, last_slot(Q, HALF), last_plane(Q, HALF))
         x_words[1, 0] = sb([P, HALF], U32, "x_words1_0")
-        move16(False, last_slot(HALF, HALF + Q), last[HALF][:])
+        move16(False, last_slot(HALF, HALF + Q), last_plane(HALF, HALF + Q))
         quantize_x(1, 0)
-        move16(False, last_slot(HALF + Q, S - LATE), last[HALF + Q][:, 0 : Q - LATE])
-        move16(True, last_slot(S - LATE, S), last[HALF + Q][:, Q - LATE : Q])
-        cast_w(1, 0, 4)
+        move16(True, last_slot(HALF + Q, S - LATE), last_plane(HALF + Q, S - LATE))
+        cast_w(1)
+        late = at(8192 + 2048, [P, LATE * PACK], BF16, "late")
+        nc.scalar.copy(
+            out=late[:].rearrange("p (c i t) -> p c t i", i=RUN, t=PACK),
+            in_=planes[1, 1][:, :, HALF - LATE : HALF].rearrange("p t (c i) -> p c t i", i=RUN),
+        )
         quantize_w(1, 0, 1)
         quantize_w(1, 1, 2)
         quantize_w(1, 2, 4)
         x_words[1, 1] = at(8192, [P, HALF], U32, "x_words1_1")
-        quantize_x(1, 1)
-        for h in range(2):
-            for t in range(PACK):
-                first_product(1, t, h)
+        for a, b, src in ((0, HALF - LATE, woven[1, 1][:, 0 : PACK * (HALF - LATE)]), (HALF - LATE, HALF, late[:])):
+            nc.vector.quantize_mx(out=x_words[1, 1][:, a:b].bitcast(FP8X4), scales=x_bytes[1, 1][:, a:b], in_=src)
+        for t in range(PACK):
+            first_product(1, t, 0)
+        for t in HALF1_ORDER:
+            first_product(1, t, 1)
 
         h_sb = [sb([P, PACK, HALF], F32, f"h_sb{h}") for h in range(2)]
         sums = [sb([P, PACK], F32, f"sums{h}") for h in range(2)]
         neg_mean = sb([P, 1, PACK, 1], F32, "neg_mean")
-        for h in range(2):
+        share = sb([P, PACK], F32, "share")
+
+        def empty(t, h):
             scale = 1.0 if h == 0 else -1.0 / S
-            for t in range(PACK):
-                if (t, h) in ON_VECTOR:
-                    nc.vector.tensor_scalar(
-                        out=h_sb[h][:, t, :], in0=banks[t, h][:], scalar1=scale, scalar2=None,
-                        op0=ALU.mult, op1=ALU.add, accum_out=sums[h][:, t : t + 1],
-                    )
-                else:
-                    nc.scalar.activation(out=h_sb[h][:, t, :], in_=banks[t, h][:], func=ACT.Copy, scale=scale, accum_out=sums[h][:, t : t + 1])
-        for t0 in (0, 2):
-            nc.vector.scalar_tensor_tensor(
-                out=neg_mean[:, 0, t0 : t0 + 2, 0], in0=sums[0][:, t0 : t0 + 2], scalar=-1.0 / S, in1=sums[1][:, t0 : t0 + 2],
-                op0=ALU.mult, op1=ALU.add,
-            )
+            folded = h == 1 and t in FOLDED
+            total = neg_mean[:, 0, t, :] if folded else sums[h][:, t : t + 1]
+            if (t, h) in ON_VECTOR and folded:
+                nc.vector.scalar_tensor_tensor(
+                    out=h_sb[h][:, t, :], in0=banks[t, h][:], scalar=scale, in1=share[:, t : t + 1].to_broadcast([P, HALF]),
+                    op0=ALU.mult, op1=ALU.add, accum_out=total,
+                )
+            elif (t, h) in ON_VECTOR:
+                nc.vector.tensor_scalar(
+                    out=h_sb[h][:, t, :], in0=banks[t, h][:], scalar1=scale, scalar2=None,
+                    op0=ALU.mult, op1=ALU.add, accum_out=total,
+                )
+            elif folded:
+                nc.scalar.activation(out=h_sb[h][:, t, :], in_=banks[t, h][:], func=ACT.Identity, scale=scale, bias=share[:, t : t + 1], accum_out=total)
+            else:
+                nc.scalar.activation(out=h_sb[h][:, t, :], in_=banks[t, h][:], func=ACT.Copy, scale=scale, accum_out=total)
+            if h == 0 and t in FOLDED:
+                nc.gpsimd.tensor_scalar(
+                    out=share[:, t : t + 1], in0=sums[0][:, t : t + 1], scalar1=-1.0 / (S * HALF), scalar2=0.0, op0=ALU.mult, op1=ALU.add
+                )
+
+        for t in range(PACK):
+            empty(t, 0)
+        for t in HALF1_ORDER:
+            empty(t, 1)
+        nc.vector.scalar_tensor_tensor(
+            out=neg_mean[:, 0, 0:PACK:3, 0], in0=sums[0][:, 0:PACK:3], scalar=-1.0 / S, in1=sums[1][:, 0:PACK:3],
+            op0=ALU.mult, op1=ALU.add,
+        )
 
         z_grouped = {}
         z_planes = {}
@@ -217,8 +247,11 @@ def tile_picked_deepset_none_e_kernel(tc, xT, w1, w2_words, w2_scales, offs, out
             z_grouped[n] = sb([P, width, PACK], BF16, f"z_grouped{n}")
             if on_scalar:
                 z_planes[n] = sb([P, PACK, width], BF16, f"z_planes{n}")
-                for t in range(PACK):
-                    nc.scalar.activation(out=z_planes[n][:, t, :], in_=src[:, t, :], func=ACT.Identity, bias=neg_mean[:, 0, t, :], scale=(1.0 if c0 < HALF else -float(S)))
+                for t in (1, 2, 0, 3):
+                    if c0 >= HALF and t in FOLDED:
+                        nc.scalar.activation(out=z_planes[n][:, t, :], in_=banks[t, 1][:, c0 - HALF : c0 - HALF + width], func=ACT.Identity, bias=neg_mean[:, 0, t, :], scale=1.0)
+                    else:
+                        nc.scalar.activation(out=z_planes[n][:, t, :], in_=src[:, t, :], func=ACT.Identity, bias=neg_mean[:, 0, t, :], scale=(1.0 if c0 < HALF else -float(S)))
             else:
                 nc.vector.tensor_tensor(
                     out=z_grouped[n][:].rearrange("p (c i) t -> p c t i", i=RUN),
@@ -242,7 +275,7 @@ def tile_picked_deepset_none_e_kernel(tc, xT, w1, w2_words, w2_scales, offs, out
             nc.vector.quantize_mx(
                 out=z_words[:].bitcast(FP8X4), scales=z_bytes[:], in_=z_grouped[n][:].rearrange("p w t -> p (w t)")
             )
-            result = psum.tile([P, HALF], F32, name=f"result{n}", tag=f"bank{n}")
+            result = psum.tile([P, HALF], F32, name=f"result{n}", tag=f"bank{RESULT_BANKS[n]}")
             nc.tensor.matmul_mx(
                 out=result[:, 0:width],
                 lhsT=w2_codes[:].bitcast(FP4X4),

@@ -24,11 +24,11 @@ HALF = 512
 Q = 256
 RUN = 4
 LATE = 128
-ON_VECTOR = ((1, 0), (3, 0), (0, 1), (2, 1))
-HALF1_ORDER = (0, 3, 2, 1)
-FOLDED = (1, 2)
-RESULT_BANKS = (0, 2, 4, 6, 1)
-W_ON_VECTOR = (84, 92)
+ON_VECTOR = ((1, 0), (3, 0), (3, 1), (2, 1))
+HALF1_ORDER = (0, 3, 1, 2)
+FOLDED = (0, 1, 2)
+RESULT_BANKS = (0, 2, 4, 6, 0)
+W_ON_VECTOR = (84, 88)
 Z_CHUNKS = [(0, 256, False), (256, 128, False), (512, 256, True), (768, 256, True), (384, 128, True)]
 
 
@@ -173,8 +173,9 @@ def tile_picked_deepset_none_e_kernel(tc, xT, w1, w2_words, w2_scales, offs, out
             return planes[1, h][:, PACK - 1, a - HALF * h : b - HALF * h]
 
         gather(False, 1, PACK - 1, last_slot(0, Q), 0, Q)
-        for a in range(Q, S, Q):
-            gather(True, 1, PACK - 1, last_plane(a, a + Q), a, a + Q)
+        cuts = (Q, HALF, HALF + Q, S - LATE, S)
+        for a, b in zip(cuts, cuts[1:]):
+            gather(True, 1, PACK - 1, last_plane(a, b), a, b)
         move16(False, last_slot(Q, HALF), last_plane(Q, HALF))
         x_words[1, 0] = sb([P, HALF], U32, "x_words1_0")
         move16(False, last_slot(HALF, HALF + Q), last_plane(HALF, HALF + Q))
@@ -199,7 +200,8 @@ def tile_picked_deepset_none_e_kernel(tc, xT, w1, w2_words, w2_scales, offs, out
 
         h_sb = [sb([P, PACK, HALF], F32, f"h_sb{h}") for h in range(2)]
         sums = [sb([P, PACK], F32, f"sums{h}") for h in range(2)]
-        neg_mean = sb([P, 1, PACK, 1], F32, "neg_mean")
+        means = sb([P, 1, PACK, 8], F32, "means")
+        neg_mean = means[:, :, :, 0:1]
         share = sb([P, PACK], F32, "share")
 
         def empty(t, h):
@@ -211,6 +213,8 @@ def tile_picked_deepset_none_e_kernel(tc, xT, w1, w2_words, w2_scales, offs, out
                     out=h_sb[h][:, t, :], in0=banks[t, h][:], scalar=scale, in1=share[:, t : t + 1].to_broadcast([P, HALF]),
                     op0=ALU.mult, op1=ALU.add, accum_out=total,
                 )
+            elif (t, h) in ON_VECTOR and h == 1:
+                nc.vector.tensor_reduce(out=total, in_=banks[t, h][:], axis=mybir.AxisListType.X, op=ALU.add)
             elif (t, h) in ON_VECTOR:
                 nc.vector.tensor_scalar(
                     out=h_sb[h][:, t, :], in0=banks[t, h][:], scalar1=scale, scalar2=None,
@@ -229,9 +233,8 @@ def tile_picked_deepset_none_e_kernel(tc, xT, w1, w2_words, w2_scales, offs, out
             empty(t, 0)
         for t in HALF1_ORDER:
             empty(t, 1)
-        nc.vector.scalar_tensor_tensor(
-            out=neg_mean[:, 0, 0:PACK:3, 0], in0=sums[0][:, 0:PACK:3], scalar=-1.0 / S, in1=sums[1][:, 0:PACK:3],
-            op0=ALU.mult, op1=ALU.add,
+        nc.gpsimd.tensor_scalar(
+            out=neg_mean[:, 0, 3, :], in0=sums[0][:, 3:4], scalar1=sums[1][:, 3:4], scalar2=-1.0 / S, op0=ALU.add, op1=ALU.mult
         )
 
         z_grouped = {}
@@ -241,28 +244,32 @@ def tile_picked_deepset_none_e_kernel(tc, xT, w1, w2_words, w2_scales, offs, out
             c0, width, on_scalar = Z_CHUNKS[n]
             return h_sb[c0 // HALF][:, :, c0 % HALF : c0 % HALF + width]
 
+        planes_z = sb([P, PACK, HALF], BF16, "planes_z")
+
         def subtract(n):
             c0, width, on_scalar = Z_CHUNKS[n]
             src = source(n)
             z_grouped[n] = sb([P, width, PACK], BF16, f"z_grouped{n}")
-            if on_scalar:
-                z_planes[n] = sb([P, PACK, width], BF16, f"z_planes{n}")
-                for t in (1, 2, 0, 3):
-                    if c0 >= HALF and t in FOLDED:
-                        nc.scalar.activation(out=z_planes[n][:, t, :], in_=banks[t, 1][:, c0 - HALF : c0 - HALF + width], func=ACT.Identity, bias=neg_mean[:, 0, t, :], scale=1.0)
-                    else:
-                        nc.scalar.activation(out=z_planes[n][:, t, :], in_=src[:, t, :], func=ACT.Identity, bias=neg_mean[:, 0, t, :], scale=(1.0 if c0 < HALF else -float(S)))
+            if on_scalar and c0 >= HALF:
+                z_planes[n] = planes_z[:, :, c0 - HALF : c0 - HALF + width]
+            elif on_scalar:
+                z_planes[n] = sb([P, PACK, width], BF16, f"z_planes{n}")[:]
+                for t in HALF1_ORDER:
+                    nc.scalar.activation(out=z_planes[n][:, t, :], in_=src[:, t, :], func=ACT.Identity, bias=neg_mean[:, 0, t, :], scale=1.0)
             else:
                 nc.vector.tensor_tensor(
                     out=z_grouped[n][:].rearrange("p (c i) t -> p c t i", i=RUN),
                     in0=src.rearrange("p t (c i) -> p c t i", i=RUN),
-                    in1=neg_mean[:].to_broadcast([P, width // RUN, PACK, RUN]),
+                    in1=neg_mean.to_broadcast([P, width // RUN, PACK, RUN]),
                     op=ALU.add,
                 )
 
-        def lay(n, on_scalar):
-            dst = z_grouped[n][:].rearrange("p (c i) j -> p c j i", i=RUN)
-            src = z_planes[n][:].rearrange("p j (c i) -> p c j i", i=RUN)
+        for t in HALF1_ORDER:
+            nc.scalar.activation(out=planes_z[:, t, :], in_=banks[t, 1][:], func=ACT.Identity, bias=neg_mean[:, 0, t, :], scale=1.0)
+
+        def lay(n, on_scalar, a, b):
+            dst = z_grouped[n][:, a:b].rearrange("p (c i) j -> p c j i", i=RUN)
+            src = z_planes[n][:, :, a:b].rearrange("p j (c i) -> p c j i", i=RUN)
             if on_scalar:
                 nc.scalar.copy(out=dst, in_=src)
             else:
@@ -292,9 +299,10 @@ def tile_picked_deepset_none_e_kernel(tc, xT, w1, w2_words, w2_scales, offs, out
 
         for n in range(len(Z_CHUNKS)):
             subtract(n)
-        lay(4, True)
+        lay(3, True, 160, 256)
+        lay(4, True, 0, 128)
         second_product(0)
-        lay(2, False)
-        lay(3, False)
+        lay(2, False, 0, 256)
+        lay(3, False, 0, 160)
         for n in (2, 3, 1, 4):
             second_product(n)

@@ -24,9 +24,9 @@ HALF = 512
 Q = 256
 RUN = 4
 LATE = 128
-ON_VECTOR = ((1, 0), (3, 0), (3, 1), (2, 1))
-HALF1_ORDER = (0, 3, 1, 2)
-FOLDED = (0, 1, 2)
+ON_VECTOR = ((1, 0), (3, 0), (3, 1), (1, 1))
+HALF1_ORDER = (2, 3, 0, 1)
+FOLDED = (0, 1)
 RESULT_BANKS = (0, 2, 4, 6, 0)
 W_ON_VECTOR = (84, 88)
 Z_CHUNKS = [(0, 256, False), (256, 128, False), (512, 256, True), (768, 256, True), (384, 128, True)]
@@ -200,8 +200,7 @@ def tile_picked_deepset_none_e_kernel(tc, xT, w1, w2_words, w2_scales, offs, out
 
         h_sb = [sb([P, PACK, HALF], F32, f"h_sb{h}") for h in range(2)]
         sums = [sb([P, PACK], F32, f"sums{h}") for h in range(2)]
-        means = sb([P, 1, PACK, 8], F32, "means")
-        neg_mean = means[:, :, :, 0:1]
+        neg_mean = sb([P, 1, PACK, 1], F32, "neg_mean")
         share = sb([P, PACK], F32, "share")
 
         def empty(t, h):
@@ -213,8 +212,6 @@ def tile_picked_deepset_none_e_kernel(tc, xT, w1, w2_words, w2_scales, offs, out
                     out=h_sb[h][:, t, :], in0=banks[t, h][:], scalar=scale, in1=share[:, t : t + 1].to_broadcast([P, HALF]),
                     op0=ALU.mult, op1=ALU.add, accum_out=total,
                 )
-            elif (t, h) in ON_VECTOR and h == 1:
-                nc.vector.tensor_reduce(out=total, in_=banks[t, h][:], axis=mybir.AxisListType.X, op=ALU.add)
             elif (t, h) in ON_VECTOR:
                 nc.vector.tensor_scalar(
                     out=h_sb[h][:, t, :], in0=banks[t, h][:], scalar1=scale, scalar2=None,
@@ -233,9 +230,8 @@ def tile_picked_deepset_none_e_kernel(tc, xT, w1, w2_words, w2_scales, offs, out
             empty(t, 0)
         for t in HALF1_ORDER:
             empty(t, 1)
-        nc.gpsimd.tensor_scalar(
-            out=neg_mean[:, 0, 3, :], in0=sums[0][:, 3:4], scalar1=sums[1][:, 3:4], scalar2=-1.0 / S, op0=ALU.add, op1=ALU.mult
-        )
+        for t in (2, 3):
+            nc.scalar.activation(out=neg_mean[:, 0, t, :], in_=sums[0][:, t : t + 1], func=ACT.Identity, scale=-1.0 / S, bias=sums[1][:, t : t + 1])
 
         z_grouped = {}
         z_planes = {}
@@ -254,18 +250,18 @@ def tile_picked_deepset_none_e_kernel(tc, xT, w1, w2_words, w2_scales, offs, out
                 z_planes[n] = planes_z[:, :, c0 - HALF : c0 - HALF + width]
             elif on_scalar:
                 z_planes[n] = sb([P, PACK, width], BF16, f"z_planes{n}")[:]
-                for t in HALF1_ORDER:
+                for t in range(PACK):
                     nc.scalar.activation(out=z_planes[n][:, t, :], in_=src[:, t, :], func=ACT.Identity, bias=neg_mean[:, 0, t, :], scale=1.0)
             else:
                 nc.vector.tensor_tensor(
                     out=z_grouped[n][:].rearrange("p (c i) t -> p c t i", i=RUN),
                     in0=src.rearrange("p t (c i) -> p c t i", i=RUN),
-                    in1=neg_mean.to_broadcast([P, width // RUN, PACK, RUN]),
+                    in1=neg_mean[:].to_broadcast([P, width // RUN, PACK, RUN]),
                     op=ALU.add,
                 )
 
-        for t in HALF1_ORDER:
-            nc.scalar.activation(out=planes_z[:, t, :], in_=banks[t, 1][:], func=ACT.Identity, bias=neg_mean[:, 0, t, :], scale=1.0)
+        for t, a, b in ((0, 0, HALF), (2, 0, HALF), (3, 0, Q), (1, 0, Q), (3, Q, HALF), (1, Q, HALF)):
+            nc.scalar.activation(out=planes_z[:, t, a:b], in_=banks[t, 1][:, a:b], func=ACT.Identity, bias=neg_mean[:, 0, t, :], scale=1.0)
 
         def lay(n, on_scalar, a, b):
             dst = z_grouped[n][:, a:b].rearrange("p (c i) j -> p c j i", i=RUN)
@@ -299,10 +295,9 @@ def tile_picked_deepset_none_e_kernel(tc, xT, w1, w2_words, w2_scales, offs, out
 
         for n in range(len(Z_CHUNKS)):
             subtract(n)
-        lay(3, True, 160, 256)
         lay(4, True, 0, 128)
         second_product(0)
         lay(2, False, 0, 256)
-        lay(3, False, 0, 160)
+        lay(3, False, 0, 256)
         for n in (2, 3, 1, 4):
             second_product(n)

from contextlib import ExitStack

import concourse.mybir as mybir

K, T, S, H, N = 1024, 2048, 1024, 512, 128
FLOPS = 2 * K * H * S + 2 * H * N * S

F32 = mybir.dt.float32
BF16 = mybir.dt.bfloat16
U32 = mybir.dt.uint32
I32 = mybir.dt.int32
U16 = mybir.dt.uint16
U8 = mybir.dt.uint8
FP8X4 = mybir.dt.float8_e4m3fn_x4
FP4X4 = mybir.dt.float4_e2m1fn_x4
ACT = mybir.ActivationFunctionType
ALU = mybir.AluOpType

P = 128
PACK = 4
K_PASS = P * PACK
PASSES = K // K_PASS
HALF = 512
Q = 256
RUN = 4
LATE = 128
ON_VECTOR = ((1, 0), (3, 0), (3, 1), (1, 1))
HALF1_ORDER = (2, 3, 0, 1)
FOLDED = (0, 1)
RESULT_BANKS = (0, 2, 4, 6, 0)
W_ON_VECTOR = (84, 88)
Z_CHUNKS = [(0, 256, False), (256, 128, False), (512, 256, True), (768, 256, True), (384, 128, True)]


def tile_picked_deepset_none_e_kernel(tc, xT, w1, w2_words, w2_scales, offs, out):
    nc = tc.nc
    with ExitStack() as ctx:
        keep = ctx.enter_context(tc.tile_pool(name="keep", bufs=1))
        shared = ctx.enter_context(tc.tile_pool(name="shared", bufs=1))
        psum = ctx.enter_context(tc.psum_pool(name="psum", bufs=1))

        def sb(shape, dtype, name):
            return keep.tile(shape, dtype, name=name, tag=name, align_bytes=64)

        def at(offset, shape, dtype, name):
            return shared.tile(shape, dtype, name=name, tag=name, align_bytes=64, offset=offset)

        offsets = keep.tile([P, S // 16], U16, name="offsets")
        w2_plane = sb([P, N], U8, "w2_plane")
        w2_codes = sb([P, 2 * N], U8, "w2_codes")
        nc.vector.memset(w2_plane[:].bitcast(U32), 0)

        x_raw = {}
        w_raw = {}

        def load_x(g, j):
            rows = xT[g * K_PASS : (g + 1) * K_PASS, :].rearrange("(p j) w -> p j w", j=PACK)
            x_raw[g, j] = sb([P, T], F32, f"x_raw{g}_{j}")
            nc.sync.dma_start(out=x_raw[g, j][:], in_=rows[:, j, :])

        def load_w(g):
            rows = w1[g * K_PASS : (g + 1) * K_PASS, :].rearrange("(p j) w -> p (j w)", j=PACK)
            w_raw[g] = at(8192 * g, [P, PACK * H], F32, f"w_raw{g}")
            nc.sync.dma_start(out=w_raw[g][:], in_=rows)

        load_x(0, 0)
        nc.sync.dma_start(offsets[:], offs)
        for j in range(1, PACK):
            load_x(0, j)
        for j in range(PACK - 1):
            load_x(1, j)
        load_w(0)
        load_x(1, PACK - 1)
        load_w(1)
        nc.sync.dma_start(out=w2_codes[:].bitcast(I32), in_=w2_words[0].bitcast(I32))
        for q in range(4):
            nc.sync.dma_start(
                out=w2_plane[32 * q : 32 * q + 4, :].bitcast(I32),
                in_=w2_scales[0, 4 * q : 4 * q + 4, :].bitcast(I32),
            )

        def move(on_scalar, dst, src):
            if on_scalar:
                nc.scalar.activation(out=dst, in_=src, func=ACT.Copy)
            else:
                nc.vector.tensor_copy(out=dst, in_=src)

        def move16(on_scalar, dst, src):
            if on_scalar:
                nc.scalar.copy(out=dst, in_=src)
            else:
                nc.vector.tensor_copy(out=dst, in_=src)

        planes = {(g, h): sb([P, PACK, HALF], BF16, f"planes{g}_{h}") for g in range(PASSES) for h in range(2)}
        woven = {(g, h): sb([P, HALF * PACK], BF16, f"woven{g}_{h}") for g in range(PASSES) for h in range(2)}
        x_words = {}
        x_bytes = {(g, h): sb([P, HALF], U8, f"x_bytes{g}_{h}") for g in range(PASSES) for h in range(2)}
        w_grouped = [sb([P, PACK, P, PACK], BF16, f"w_grouped{g}") for g in range(PASSES)]
        w_words = [sb([P, H], U32, f"w_words{g}") for g in range(PASSES)]
        w_bytes = [sb([P, H], U8, f"w_bytes{g}") for g in range(PASSES)]

        def gather(on_scalar, g, j, dst, a, b):
            move(on_scalar, dst, x_raw[g, j][:].indirect(offsets[:, a // 16 : b // 16]))

        def gather_plane(g, j, on_scalar):
            for h in range(2):
                gather(on_scalar[h], g, j, planes[g, h][:, j, :], HALF * h, HALF * (h + 1))

        def lay_planes(on_scalar, g, h, a, b):
            rows = PACK - g
            dst = woven[g, h][:, PACK * a : PACK * b].rearrange("p (c i t) -> p c t i", i=RUN, t=PACK)[:, :, 0:rows, :]
            src = planes[g, h][:, 0:rows, a:b].rearrange("p t (c i) -> p c t i", i=RUN)
            move16(on_scalar, dst, src)

        def last_slot(a, b):
            h = a // HALF
            return woven[1, h][:].rearrange("p (c t) -> p c t", t=PACK)[:, a - HALF * h : b - HALF * h, PACK - 1]

        def quantize_x(g, h):
            nc.vector.quantize_mx(out=x_words[g, h][:].bitcast(FP8X4), scales=x_bytes[g, h][:], in_=woven[g, h][:])

        def cast_w(g):
            src = w_raw[g][:].rearrange("p (j m t) -> p m j t", j=PACK, t=PACK)
            dst = w_grouped[g][:].rearrange("p t m j -> p m j t")
            cut = W_ON_VECTOR[g]
            move(False, dst[:, 0:cut], src[:, 0:cut])
            move(True, dst[:, cut:P], src[:, cut:P])

        def quantize_w(g, t0, t1):
            nc.vector.quantize_mx(
                out=w_words[g][:, P * t0 : P * t1].bitcast(FP8X4),
                scales=w_bytes[g][:, P * t0 : P * t1],
                in_=w_grouped[g][:, t0:t1].rearrange("p t m j -> p (t m j)"),
            )

        banks = {}

        def first_product(g, t, h):
            if g == 0:
                banks[t, h] = psum.tile([P, HALF], F32, name=f"h{t}_{h}", tag=f"bank{2 * t + h}")
            nc.tensor.matmul_mx(
                out=banks[t, h][:],
                lhsT=w_words[g][:, P * t : P * (t + 1)].bitcast(FP8X4),
                lhsT_scale=w_bytes[g][:, P * t : P * (t + 1)],
                rhs=x_words[g, h][:].bitcast(FP8X4),
                rhs_scale=x_bytes[g, h][:],
                start=(g == 0),
                stop=(g == PASSES - 1),
            )

        for j in range(PACK):
            gather_plane(0, j, (False, True))
        for h in range(2):
            lay_planes(False, 0, h, 0, HALF)
        for h in range(2):
            x_words[0, h] = sb([P, HALF], U32, f"x_words0_{h}")
            quantize_x(0, h)
        gather_plane(1, 0, (True, True))
        gather_plane(1, 1, (False, True))
        gather_plane(1, 2, (False, True))
        lay_planes(False, 1, 0, 0, HALF)
        lay_planes(False, 1, 1, 0, LATE)
        lay_planes(True, 1, 1, LATE, HALF - LATE)
        cast_w(0)
        quantize_w(0, 0, 2)
        quantize_w(0, 2, 4)
        for t in range(PACK):
            for h in range(2):
                first_product(0, t, h)

        def last_plane(a, b):
            h = a // HALF
            return planes[1, h][:, PACK - 1, a - HALF * h : b - HALF * h]

        gather(False, 1, PACK - 1, last_slot(0, Q), 0, Q)
        cuts = (Q, HALF, HALF + Q, S - LATE, S)
        for a, b in zip(cuts, cuts[1:]):
            gather(True, 1, PACK - 1, last_plane(a, b), a, b)
        move16(False, last_slot(Q, HALF), last_plane(Q, HALF))
        x_words[1, 0] = sb([P, HALF], U32, "x_words1_0")
        move16(False, last_slot(HALF, HALF + Q), last_plane(HALF, HALF + Q))
        quantize_x(1, 0)
        move16(True, last_slot(HALF + Q, S - LATE), last_plane(HALF + Q, S - LATE))
        cast_w(1)
        late = at(8192 + 2048, [P, LATE * PACK], BF16, "late")
        nc.scalar.copy(
            out=late[:].rearrange("p (c i t) -> p c t i", i=RUN, t=PACK),
            in_=planes[1, 1][:, :, HALF - LATE : HALF].rearrange("p t (c i) -> p c t i", i=RUN),
        )
        quantize_w(1, 0, 1)
        quantize_w(1, 1, 2)
        quantize_w(1, 2, 4)
        x_words[1, 1] = at(8192, [P, HALF], U32, "x_words1_1")
        for a, b, src in ((0, HALF - LATE, woven[1, 1][:, 0 : PACK * (HALF - LATE)]), (HALF - LATE, HALF, late[:])):
            nc.vector.quantize_mx(out=x_words[1, 1][:, a:b].bitcast(FP8X4), scales=x_bytes[1, 1][:, a:b], in_=src)
        for t in range(PACK):
            first_product(1, t, 0)
        for t in HALF1_ORDER:
            first_product(1, t, 1)

        h_sb = [sb([P, PACK, HALF], F32, f"h_sb{h}") for h in range(2)]
        sums = [sb([P, PACK], F32, f"sums{h}") for h in range(2)]
        neg_mean = sb([P, 1, PACK, 1], F32, "neg_mean")
        share = sb([P, PACK], F32, "share")

        def empty(t, h):
            scale = 1.0 if h == 0 else -1.0 / S
            folded = h == 1 and t in FOLDED
            total = neg_mean[:, 0, t, :] if folded else sums[h][:, t : t + 1]
            if (t, h) in ON_VECTOR and folded:
                nc.vector.scalar_tensor_tensor(
                    out=h_sb[h][:, t, :], in0=banks[t, h][:], scalar=scale, in1=share[:, t : t + 1].to_broadcast([P, HALF]),
                    op0=ALU.mult, op1=ALU.add, accum_out=total,
                )
            elif (t, h) in ON_VECTOR:
                nc.vector.tensor_scalar(
                    out=h_sb[h][:, t, :], in0=banks[t, h][:], scalar1=scale, scalar2=None,
                    op0=ALU.mult, op1=ALU.add, accum_out=total,
                )
            elif folded:
                nc.scalar.activation(out=h_sb[h][:, t, :], in_=banks[t, h][:], func=ACT.Identity, scale=scale, bias=share[:, t : t + 1], accum_out=total)
            else:
                nc.scalar.activation(out=h_sb[h][:, t, :], in_=banks[t, h][:], func=ACT.Copy, scale=scale, accum_out=total)
            if h == 0 and t in FOLDED:
                nc.gpsimd.tensor_scalar(
                    out=share[:, t : t + 1], in0=sums[0][:, t : t + 1], scalar1=-1.0 / (S * HALF), scalar2=0.0, op0=ALU.mult, op1=ALU.add
                )

        for t in range(PACK):
            empty(t, 0)
        for t in HALF1_ORDER:
            empty(t, 1)
        for t in (2, 3):
            nc.scalar.activation(out=neg_mean[:, 0, t, :], in_=sums[0][:, t : t + 1], func=ACT.Identity, scale=-1.0 / S, bias=sums[1][:, t : t + 1])

        z_grouped = {}
        z_planes = {}

        def source(n):
            c0, width, on_scalar = Z_CHUNKS[n]
            return h_sb[c0 // HALF][:, :, c0 % HALF : c0 % HALF + width]

        planes_z = sb([P, PACK, HALF], BF16, "planes_z")

        def subtract(n):
            c0, width, on_scalar = Z_CHUNKS[n]
            src = source(n)
            z_grouped[n] = sb([P, width, PACK], BF16, f"z_grouped{n}")
            if on_scalar and c0 >= HALF:
                z_planes[n] = planes_z[:, :, c0 - HALF : c0 - HALF + width]
            elif on_scalar:
                z_planes[n] = sb([P, PACK, width], BF16, f"z_planes{n}")[:]
                for t in range(PACK):
                    nc.scalar.activation(out=z_planes[n][:, t, :], in_=src[:, t, :], func=ACT.Identity, bias=neg_mean[:, 0, t, :], scale=1.0)
            else:
                nc.vector.tensor_tensor(
                    out=z_grouped[n][:].rearrange("p (c i) t -> p c t i", i=RUN),
                    in0=src.rearrange("p t (c i) -> p c t i", i=RUN),
                    in1=neg_mean[:].to_broadcast([P, width // RUN, PACK, RUN]),
                    op=ALU.add,
                )

        for t, a, b in ((0, 0, HALF), (2, 0, HALF), (3, 0, Q), (1, 0, Q), (3, Q, HALF), (1, Q, HALF)):
            nc.scalar.activation(out=planes_z[:, t, a:b], in_=banks[t, 1][:, a:b], func=ACT.Identity, bias=neg_mean[:, 0, t, :], scale=1.0)

        def lay(n, on_scalar, a, b):
            dst = z_grouped[n][:, a:b].rearrange("p (c i) j -> p c j i", i=RUN)
            src = z_planes[n][:, :, a:b].rearrange("p j (c i) -> p c j i", i=RUN)
            if on_scalar:
                nc.scalar.copy(out=dst, in_=src)
            else:
                nc.vector.tensor_copy(out=dst, in_=src)

        def second_product(n):
            c0, width, on_scalar = Z_CHUNKS[n]
            z_words = sb([P, width], U32, f"z_words{n}")
            z_bytes = sb([P, width], U8, f"z_bytes{n}")
            nc.vector.quantize_mx(
                out=z_words[:].bitcast(FP8X4), scales=z_bytes[:], in_=z_grouped[n][:].rearrange("p w t -> p (w t)")
            )
            result = psum.tile([P, HALF], F32, name=f"result{n}", tag=f"bank{RESULT_BANKS[n]}")
            nc.tensor.matmul_mx(
                out=result[:, 0:width],
                lhsT=w2_codes[:].bitcast(FP4X4),
                lhsT_scale=w2_plane[:],
                rhs=z_words[:].bitcast(FP8X4),
                rhs_scale=z_bytes[:],
                start=True,
                stop=True,
            )
            staged = sb([P, width], F32, f"staged{n}")
            move(n != 1, staged[:], result[:, 0:width])
            queue = nc.scalar if n == len(Z_CHUNKS) - 1 else nc.sync
            queue.dma_start(out=out[:, c0 : c0 + width], in_=staged[:])

        for n in range(len(Z_CHUNKS)):
            subtract(n)
        lay(4, True, 0, 128)
        second_product(0)
        lay(2, False, 0, 256)
        lay(3, False, 0, 256)
        for n in (2, 3, 1, 4):
            second_product(n)
